import numpy as np
import ml_dtypes


def mxq(x, axis, fmt="e4m3"):
    dtype, down = {"e4m3": (ml_dtypes.float8_e4m3fn, 7), "e5m2": (ml_dtypes.float8_e5m2, 14)}[fmt]
    v = np.moveaxis(np.asarray(x, np.float32).astype(ml_dtypes.bfloat16).astype(np.float64), axis, -1)
    blocks = v.reshape(v.shape[:-1] + (-1, 32))
    amax = np.abs(blocks).max(-1, keepdims=True)
    byte = np.maximum(np.where(amax > 0, np.frexp(amax)[1] - 1 + 127, 0) - down, 1)
    scale = np.exp2(byte - 127.0)
    codes = (blocks / scale).astype(np.float32).astype(dtype).astype(np.float64)
    return np.moveaxis((codes * scale).reshape(v.shape), -1, axis)


WIDE = False


def mx_kscale(k):
    if not WIDE:
        return np.ones(k)
    levels = np.array([10, -10, 5, -5, 0])
    if k % 512:
        return np.exp2(np.random.permutation(np.resize(levels, k // 32))).repeat(32)
    a = np.empty((k // 512, 16))
    for p in range(k // 512):
        a[p, :8] = np.random.permutation(np.resize(levels, 8))
        for g in range(8):
            far = levels[np.abs(levels - a[p, g]) >= 10]
            a[p, g + 8] = far[np.random.randint(len(far))]
    return np.exp2(a.ravel()).repeat(32)


def f64(x):
    return np.asarray(x).astype(np.float64)


def striped(idx):
    return np.tile(idx.reshape(-1, 16).T, (8, 1)).astype(np.uint16)


def unstriped(offs):
    return offs[:16].T.reshape(-1).astype(np.int64)


E2M1 = np.array([0.0, 0.5, 1.0, 1.5, 2.0, 3.0, 4.0, 6.0, -0.0, -0.5, -1.0, -1.5, -2.0, -3.0, -4.0, -6.0])


def pack_weight(w, fmt):
    k, n = w.shape
    w = f64(np.asarray(w, np.float32).astype(ml_dtypes.bfloat16)).reshape(k // 32, 32, n)
    amax = np.abs(w).max(1)
    if fmt == "e4m3":
        byte = np.frexp(amax)[1] - 1 + 127 - 7
    else:
        mant, ex = np.frexp(amax / 6.0)
        byte = np.where(mant > 0.5, ex, ex - 1) + 127
    byte = np.clip(np.where(amax > 0, byte, 1), 1, 254)
    scaled = (w * np.exp2(127.0 - byte)[:, None, :]).reshape(k, n).astype(np.float32)
    by_word = np.ascontiguousarray(scaled.reshape(k // 512, 128, 4, n).transpose(0, 1, 3, 2))
    if fmt == "e4m3":
        words = by_word.astype(ml_dtypes.float8_e4m3fn).view(np.uint8)
    else:
        c = by_word.astype(ml_dtypes.float4_e2m1fn).view(np.uint8) & 0xF
        words = (c[..., 0::2] | (c[..., 1::2] << 4)).reshape(k // 512, 128, 2 * n)
    return np.ascontiguousarray(words), np.ascontiguousarray(byte.astype(np.uint8).reshape(k // 512, 16, n))


def unpack_weight(words, scales, fmt):
    g, _, n = scales.shape
    words = np.ascontiguousarray(words).reshape(g, 128, n, -1)
    if fmt == "e4m3":
        vals = words.view(ml_dtypes.float8_e4m3fn).astype(np.float64)
    else:
        nib = np.empty((g, 128, n, 4), np.uint8)
        nib[..., 0::2] = words & 0xF
        nib[..., 1::2] = words >> 4
        vals = E2M1[nib]
    vals = vals * np.repeat(np.exp2(scales.astype(np.float64) - 127.0), 8, axis=1)[..., None]
    return vals.transpose(0, 1, 3, 2).reshape(g * 512, n)


def gelu(v):
    return 0.5 * v * (1.0 + np.tanh(np.sqrt(2.0 / np.pi) * (v + 0.044715 * v**3)))


K, H, N, T, S, T2, P = 1536, 1024, 384, 4096, 1024, 2048, 1024


def setup_inputs():
    n = np.random.standard_normal
    s = mx_kscale(K)[:, None]
    u = mx_kscale(H)[:, None]
    tab_words, tab_scales = pack_weight(n((K, T)) * s, "e4m3")
    w4_words, w4_scales = pack_weight(n((H, N)) / np.sqrt(H) / u, "e2m1")
    w1 = n((K, H)) / np.sqrt(K) / s
    gain = np.random.choice([-1.0, 1.0], H) * np.random.uniform(0.6, 1.4, H) * u[:, 0]
    return {
        "tab_words": tab_words, "tab_scales": tab_scales,
        "offs": striped(np.random.permutation(T)[:S]),
        "w1": w1.astype(np.float32),
        "gain": gain.astype(np.float32),
        "page0": (n((H, T2)) * u).astype(np.float32),
        "wgs": np.exp(0.3 * n((128, S))).astype(np.float32),
        "offs2": striped(np.random.permutation(T2)[:S]),
        "offs3": striped(np.random.permutation(T2)[:P]),
        "offs4": striped(np.random.permutation(T2)[:P]),
        "amp": np.random.uniform(1.4, 2.6, H).astype(np.float32),
        "w4_words": w4_words, "w4_scales": w4_scales,
        "w3": (0.7 * n((H, N)) / np.sqrt(H) / u).astype(np.float32),
    }


def reference(tab_words, tab_scales, offs, w1, gain, page0, wgs, offs2, offs3, offs4,
              amp, w4_words, w4_scales, w3):
    v = unpack_weight(tab_words, tab_scales, "e4m3")[:, unstriped(offs)]
    h = f64(gain)[:, None] * np.abs(mxq(f64(w1), 0, "e4m3").T @ v)
    before = f64(page0)
    page = before.copy()
    page[:, unstriped(offs2)] = np.tile(f64(wgs), (H // 128, 1)) * h
    changed = page[:, unstriped(offs3)]
    earlier = before[:, unstriped(offs4)]
    x = f64(amp)[:, None] * changed - np.minimum(changed, earlier)
    xq = mxq(x, 0, "e4m3")
    w4 = unpack_weight(w4_words, w4_scales, "e2m1")
    bounded = np.tanh(w4.T @ xq)
    return bounded + (mxq(f64(w3), 0, "e4m3").T @ xq)

@@ -1,0 +1,387 @@
+from contextlib import ExitStack
+
+import concourse.mybir as mybir
+from concourse.masks import make_identity
+
+K, H, N, T, S, T2, M = 1536, 1024, 384, 4096, 1024, 2048, 1024
+FLOPS = 2 * K * H * S + 2 * 2 * H * N * M
+
+F32 = mybir.dt.float32
+BF16 = mybir.dt.bfloat16
+I32 = mybir.dt.int32
+U32 = mybir.dt.uint32
+U16 = mybir.dt.uint16
+U8 = mybir.dt.uint8
+FP8X4 = mybir.dt.float8_e4m3fn_x4
+FP4X4 = mybir.dt.float4_e2m1fn_x4
+ALU = mybir.AluOpType
+ACT = mybir.ActivationFunctionType
+
+P = 128
+PASS = 512
+KP = K // PASS
+HP = H // PASS
+BANK = 512
+HALF_COLS = BANK // 16
+SLICES = H // P
+LAST = SLICES - 1
+PAGE_SLOT = [0, 1, 2, 3, 4, 5, 0, 1]
+
+
+def tile_list_bridge_wear_scores_kernel(tc, tab_words, tab_scales, offs, w1, gain, page0, wgs,
+                                                  offs2, offs3, offs4, amp, w4_words, w4_scales, w3, out):
+    nc = tc.nc
+    with ExitStack() as ctx:
+        lists = ctx.enter_context(tc.tile_pool(name="lists", bufs=1))
+        sb = ctx.enter_context(tc.tile_pool(name="sb", bufs=1))
+        ps = ctx.enter_context(tc.psum_pool(name="ps", bufs=1))
+
+        def buf(shape, dtype, tag):
+            return sb.tile(shape, dtype, tag=tag, name=tag, align_bytes=64)
+
+        def bank(b):
+            return ps.tile([P, BANK], F32, tag="bank%d" % b, name="bank%d" % b)
+
+        def load_list(src, name):
+            entries = lists.tile([P, S // 16], U16, name=name)
+            nc.sync.dma_start(entries[:], src)
+            return entries
+
+        def half(h):
+            return slice(h * BANK, (h + 1) * BANK)
+
+        def half_list(entries, h):
+            return entries[:, h * HALF_COLS:(h + 1) * HALF_COLS]
+
+        def blk(i):
+            return slice(i * P, (i + 1) * P)
+
+        ident = buf([P, P], F32, "ident")
+        make_identity(nc, ident[:])
+        tab_sc = buf([P, T], U8, "tab_sc")
+        nc.vector.memset(tab_sc[:].bitcast(I32), 0)
+        rows_lo = buf([P, P], F32, "rows_lo")
+        nc.vector.memset(rows_lo[:], 0.0)
+        w4_sc = buf([P, HP * N], U8, "w4_sc")
+        nc.vector.memset(w4_sc[:].bitcast(I32), 0)
+
+        pages = {}
+
+        def load_page(s):
+            page = buf([P, T2], F32, "page%d" % PAGE_SLOT[s])
+            if s < 4:
+                src = page0[blk(s), :]
+            else:
+                src = page0[PASS:, :].rearrange("(p t) c -> p t c", t=4)[:, s - 4, :]
+            nc.sync.dma_start(out=page[:], in_=src)
+            pages[s] = page
+
+        tab = {}
+
+        def load_table(a):
+            words = buf([P, T], U32, "big%d" % a)
+            nc.sync.dma_start(out=words[:].bitcast(I32),
+                              in_=tab_words[a].rearrange("p t i -> p (t i)").bitcast(I32))
+            tab[a] = words
+
+        raw_lo = {}
+
+        def load_w1_slice(s):
+            raw = buf([P, KP, 4, P], F32, "raw%d" % (s % 3))
+            for a in range(KP):
+                rows = w1[a * PASS:(a + 1) * PASS, blk(s)]
+                nc.sync.dma_start(out=raw[:, a, :, :], in_=rows.rearrange("(p j) c -> p j c", j=4))
+            raw_lo[s] = raw
+
+        load_page(0)
+        idx4 = load_list(offs4, "idx4")
+        for q in range(4):
+            nc.sync.dma_start(out=tab_sc[32 * q:32 * q + 4 * KP, :].bitcast(I32),
+                              in_=tab_scales[:, 4 * q:4 * q + 4, :].bitcast(I32))
+        load_table(0)
+        idx = load_list(offs, "idx")
+        load_w1_slice(0)
+        nc.sync.dma_start(out=rows_lo[0:4, :], in_=gain[0:PASS].rearrange("(s p) -> s p", p=P))
+        nc.sync.dma_start(out=rows_lo[4:8, :], in_=amp[0:PASS].rearrange("(s p) -> s p", p=P))
+        load_table(1)
+        wgs_lo = buf([P, S], F32, "wgs_lo")
+        nc.sync.dma_start(out=wgs_lo[:], in_=wgs)
+        idx2 = load_list(offs2, "idx2")
+        load_table(2)
+        load_page(1)
+        load_w1_slice(1)
+        idx3 = load_list(offs3, "idx3")
+        load_w1_slice(2)
+        load_page(2)
+
+        turned = bank(6)
+        nc.tensor.transpose(turned[:, 0:P], rows_lo[:], ident[:])
+        cols_lo = buf([P, 8], F32, "cols_lo")
+        nc.scalar.copy(out=cols_lo[:], in_=turned[:, 0:8])
+        am1_lo = buf([P, 4], F32, "am1_lo")
+        nc.vector.tensor_scalar(out=am1_lo[:], in0=cols_lo[:, 4:8], scalar1=-1.0, scalar2=None, op0=ALU.add)
+
+        earlier = {}
+        after_page = {}
+        first_two = buf([P, 2 * M], F32, "page4")
+
+        def fetch_earlier(s):
+            if s < 2:
+                e = first_two[:, s * M:(s + 1) * M]
+            else:
+                e = after_page[s - 2][:, 0:M]
+            if s == LAST:
+                nc.vector.tensor_copy(out=e, in_=pages[s][:].indirect(idx4[:]))
+            else:
+                for h in range(2):
+                    nc.vector.tensor_scalar(out=e[:, half(h)], in0=pages[s][:].indirect(half_list(idx4, h)),
+                                            scalar1=-1.0, scalar2=0.0, op0=ALU.mult, op1=ALU.add)
+            earlier[s] = e
+
+        w1_codes = {}
+
+        def quantise_w1_slice(s):
+            raw = raw_lo[s]
+            grouped = buf([P, KP, P * 4], BF16, ["slot0", "ring0", "slot1", "slot2"][s])
+            for a in range(KP):
+                nc.scalar.copy(out=grouped[:, a, :].rearrange("p (c i j) -> p c j i", i=4, j=4),
+                               in_=raw[:, a, :, :].rearrange("p j (c i) -> p c j i", i=4))
+            codes = buf([P, KP * P], U32, "w1c%d" % s)
+            scales = buf([P, KP * P], U8, "w1s%d" % s)
+            nc.vector.quantize_mx(out=codes[:].bitcast(FP8X4), scales=scales[:],
+                                  in_=grouped[:].rearrange("p a w -> p (a w)"))
+            w1_codes[s] = [(codes[:, blk(a)], scales[:, blk(a)]) for a in range(KP)]
+
+        fetch_earlier(0)
+        v_sc = buf([P, S], U8, "v_sc")
+        nc.vector.tensor_copy(out=v_sc[:], in_=tab_sc[:].indirect(idx[:]))
+        v = {}
+        for a in range(KP):
+            v[a] = buf([P, S], U32, "v%d" % a)
+            if a < KP - 1:
+                nc.vector.tensor_copy(out=v[a][:], in_=tab[a][:].indirect(idx[:]))
+            else:
+                for h in range(2):
+                    nc.vector.tensor_copy(out=v[a][:, half(h)], in_=tab[a][:].indirect(half_list(idx, h)))
+            if a == 0:
+                quantise_w1_slice(0)
+
+        habs = {}
+        wg = {}
+        later = {}
+
+        def features(s):
+            hab = buf([P, S], F32, "habs%d" % (s % 3))
+            for h in range(2):
+                acc = bank(h if s == 0 else 2 + h)
+                for a in range(KP):
+                    codes, scales = w1_codes[s][a]
+                    nc.tensor.matmul_mx(out=acc[:], lhsT=codes.bitcast(FP8X4), lhsT_scale=scales,
+                                        rhs=v[a][:, half(h)].bitcast(FP8X4), rhs_scale=v_sc[4 * a:P, half(h)],
+                                        start=(a == 0), stop=(a == KP - 1))
+                nc.scalar.activation(out=hab[:, half(h)], in_=acc[:], func=ACT.Abs)
+            habs[s] = hab
+
+        def gained_weights(s):
+            w = buf([P, S], F32, "wg0")[:] if s == 0 else after_page[s - 1][:, M:]
+            if s < 4:
+                nc.scalar.activation(out=w, in_=wgs_lo[:], func=ACT.Copy, scale=cols_lo[:, s:s + 1])
+            else:
+                nc.scalar.activation(out=w, in_=later["wgs"][:, s - 4, :], func=ACT.Copy,
+                                     scale=later["gain"][:, s - 4:s - 3])
+            wg[s] = w
+
+        def put(s):
+            if s == 0:
+                for h in range(2):
+                    nc.vector.tensor_tensor(pages[s][:].indirect(half_list(idx2, h)), habs[s][:, half(h)],
+                                            wg[s][:, half(h)], ALU.mult)
+            else:
+                nc.vector.tensor_tensor(pages[s][:].indirect(idx2[:]), habs[s][:], wg[s], ALU.mult)
+
+        xq = [(buf([P, M], U32, "xq%d" % b), buf([P, M], U8, "xs%d" % b)) for b in range(HP)]
+        planes = [buf([P, 4, BANK], BF16, "plane%d" % h) for h in range(2)]
+        turned_parts = {}
+
+        def quantise_x(b, h, grouped):
+            nc.vector.quantize_mx(out=xq[b][0][:, half(h)].bitcast(FP8X4), scales=xq[b][1][:, half(h)],
+                                  in_=grouped[:].rearrange("p m t -> p (m t)"))
+
+        def add_turned(dst, first, second):
+            nc.tensor.matmul(dst, lhsT=first, rhs=ident[:], is_transpose=True, start=True, stop=False)
+            nc.tensor.matmul(dst, lhsT=second, rhs=ident[:], is_transpose=True, start=False, stop=True)
+
+        changed = {}
+
+        def fetch_changed(s):
+            c = buf([P, M], F32, "ring%d" % (s % 2))
+            nc.vector.tensor_copy(out=c[:], in_=pages[s][:].indirect(idx3[:]))
+            changed[s] = c
+            after_page[s] = buf([P, T2], F32, "page%d" % PAGE_SLOT[s])
+
+        def compare(s):
+            c = changed[s]
+            lin = buf([P, M], F32, "ring%d" % ((s + 1) % 2))
+            am1 = am1_lo[:, s:s + 1] if s < 4 else later["am1"][:, s - 4:s - 3]
+            if s == 0:
+                turned_parts["over"] = buf([P, 8, 4, P], F32, "big0")
+                turned_parts["lin"] = buf([P, 8, 4, P], F32, "big1")
+            if s >= 4:
+                turned_parts["over"] = buf([P, M], F32, "big0")
+                turned_parts["lin"] = buf([P, M], F32, "big1")
+            over_t, lin_t = turned_parts["over"], turned_parts["lin"]
+
+            def leave(dst, h, src, func):
+                if s < 4:
+                    nc.scalar.activation(out=dst[:, 4 * h:4 * h + 4, :, 32 * s:32 * s + 32],
+                                         in_=src[:].rearrange("p (b q t) -> p b t q", b=4, t=4), func=func)
+                else:
+                    nc.scalar.activation(out=dst[:, half(h)], in_=src[:], func=func)
+
+            for h in range(2):
+                nc.scalar.activation(out=lin[:, half(h)], in_=c[:, half(h)], func=ACT.Copy, scale=am1)
+            for h in range(2):
+                diff = bank(2 + h)
+                for i in range(4):
+                    add_turned(diff[:, blk(i)], earlier[s][:, blk(4 * h + i)], c[:, blk(4 * h + i)])
+                leave(over_t, h, diff, ACT.Relu)
+                lin_bank = bank(4 + h)
+                for i in range(4):
+                    nc.tensor.transpose(lin_bank[:, blk(i)], lin[:, blk(4 * h + i)], ident[:])
+                leave(lin_t, h, lin_bank, ACT.Copy)
+                if s >= 4:
+                    back = bank(6 + h)
+                    for i in range(4):
+                        add_turned(back[:, blk(i)], over_t[:, blk(4 * h + i)], lin_t[:, blk(4 * h + i)])
+                    nc.scalar.copy(out=planes[h][:, s - 4, :], in_=back[:])
+
+        def first_block_back():
+            over_t, lin_t = turned_parts["over"], turned_parts["lin"]
+            for h in range(2):
+                grouped = buf([P, BANK, 4], BF16, "slot%d" % [1, 3][h])
+                for i in range(4):
+                    mb = 4 * h + i
+                    back = bank([0, 1, 6, 7][i])
+                    for t in range(4):
+                        add_turned(back[:, blk(t)], over_t[:, mb, t, :], lin_t[:, mb, t, :])
+                    nc.scalar.copy(out=grouped[:, blk(i), :], in_=back[:].rearrange("p (t m) -> p m t", t=4))
+                quantise_x(0, h, grouped)
+
+        def compare_last(h):
+            s = LAST
+            c = buf([P, BANK], F32, ["ring1", "low0"][h])
+            nc.vector.tensor_copy(out=c[:], in_=pages[s][:].indirect(half_list(idx3, h)))
+            low = buf([P, BANK], F32, ["low0", "low1"][h])
+            nc.vector.tensor_tensor(low[:], c[:], earlier[s][:, half(h)], ALU.min)
+            nc.vector.scalar_tensor_tensor(out=planes[h][:, 3, :], in0=c[:], scalar=later["amp"][:, 3:4], in1=low[:],
+                                           op0=ALU.mult, op1=ALU.subtract)
+            grouped = buf([P, BANK, 4], BF16, "slot0")
+            weave = nc.scalar.copy if h == 0 else nc.vector.tensor_copy
+            weave(out=grouped[:].rearrange("p (c i) t -> p c t i", i=4),
+                  in_=planes[h][:].rearrange("p t (c i) -> p c t i", i=4))
+            quantise_x(1, h, grouped)
+
+        def second_block_weights():
+            gain_hi = buf([P, 4], F32, "gain_hi")
+            nc.sync.dma_start(out=gain_hi[:], in_=gain[PASS:].rearrange("(p t) -> p t", t=4))
+            amp_hi = buf([P, 4], F32, "amp_hi")
+            nc.sync.dma_start(out=amp_hi[:], in_=amp[PASS:].rearrange("(p t) -> p t", t=4))
+            am1_hi = buf([P, 3], F32, "am1_hi")
+            nc.vector.tensor_scalar(out=am1_hi[:], in0=amp_hi[:, 0:3], scalar1=-1.0, scalar2=None, op0=ALU.add)
+            passes = []
+            for a in range(KP):
+                raw = buf([P, 4, PASS], F32, "raw%d" % ((a + 1) % 3))
+                rows = w1[a * PASS:(a + 1) * PASS, PASS:]
+                nc.sync.dma_start(out=raw[:], in_=rows.rearrange("(p j) c -> p j c", j=4))
+                grouped = buf([P, PASS * 4], BF16, "slot%d" % [0, 1, 3][a])
+                nc.scalar.copy(out=grouped[:].rearrange("p (t m j) -> p m j t", t=4, j=4),
+                               in_=raw[:].rearrange("p j (m t) -> p m j t", t=4))
+                codes = buf([P, PASS], U32, "w1hc%d" % a)
+                scales = buf([P, PASS], U8, "w1hs%d" % a)
+                nc.vector.quantize_mx(out=codes[:].bitcast(FP8X4), scales=scales[:], in_=grouped[:])
+                passes.append((codes, scales))
+            for t in range(4):
+                w1_codes[4 + t] = [(codes[:, blk(t)], scales[:, blk(t)]) for codes, scales in passes]
+            load_page(3)
+            dealt = buf([P, 4, S], F32, "big2")
+            for g in range(4):
+                nc.sync.dma_start(out=dealt[32 * g:32 * g + 32, :, :], in_=wgs.rearrange("(q t) j -> q t j", t=4))
+            later["gain"] = gain_hi
+            later["amp"] = amp_hi
+            later["am1"] = am1_hi
+            later["wgs"] = dealt
+
+        w3_q = []
+        w4_w = []
+
+        def second_stage_weights():
+            for b in range(HP):
+                raw = buf([P, 4, N], F32, "raw%d" % (b + 1))
+                nc.sync.dma_start(out=raw[:], in_=w3[b * PASS:(b + 1) * PASS, :].rearrange("(p j) n -> p j n", j=4))
+                grouped = buf([P, N * 4], BF16, "slot%d" % [2, 0][b])
+                nc.scalar.copy(out=grouped[:].rearrange("p (c i j) -> p c j i", i=4, j=4),
+                               in_=raw[:].rearrange("p j (c i) -> p c j i", i=4))
+                codes = buf([P, N], U32, "w3c%d" % b)
+                scales = buf([P, N], U8, "w3s%d" % b)
+                nc.vector.quantize_mx(out=codes[:].bitcast(FP8X4), scales=scales[:], in_=grouped[:])
+                w3_q.append((codes, scales))
+                words = buf([P, 2 * N], U8, "w4w%d" % b)
+                nc.sync.dma_start(out=words[:].bitcast(I32), in_=w4_words[b].bitcast(I32))
+                w4_w.append(words)
+            for q in range(4):
+                nc.sync.dma_start(out=w4_sc[32 * q:32 * q + 4, :].bitcast(I32).rearrange("r (b n) -> r b n", b=HP),
+                                  in_=w4_scales[:, 4 * q:4 * q + 4, :].bitcast(I32).rearrange("b r n -> r b n"))
+
+        gained_weights(0)
+        features(0)
+        fetch_earlier(1)
+        quantise_w1_slice(1)
+        features(1)
+        quantise_w1_slice(2)
+        load_w1_slice(3)
+        quantise_w1_slice(3)
+        second_block_weights()
+        load_page(5)
+        for s in range(SLICES):
+            put(s)
+            if s == LAST:
+                break
+            fetch_changed(s)
+            gained_weights(s + 1)
+            if s + 2 < SLICES:
+                fetch_earlier(s + 2)
+            compare(s)
+            if s + 2 < SLICES:
+                features(s + 2)
+            if s == 3:
+                first_block_back()
+            if s == 1:
+                load_page(4)
+            if s in (2, 3):
+                load_page(s + 4)
+            if s == 2:
+                second_stage_weights()
+
+        order = [0, 1, 2, 3, 4, 5, 6, 7, 0, 1, 2, 3]
+        for h in range(2):
+            compare_last(h)
+        for h in range(2):
+            for n in range(N // P):
+                g = 2 * (h * (N // P) + n)
+                y4 = bank(order[g])
+                for b in range(HP):
+                    nc.tensor.matmul_mx(out=y4[:], lhsT=w4_w[b][:, 2 * n * P:2 * (n + 1) * P].bitcast(FP4X4),
+                                        lhsT_scale=w4_sc[:, b * N + n * P:b * N + (n + 1) * P],
+                                        rhs=xq[b][0][:, half(h)].bitcast(FP8X4), rhs_scale=xq[b][1][:, half(h)],
+                                        start=(b == 0), stop=(b == HP - 1))
+                y3 = bank(order[g + 1])
+                for b in range(HP):
+                    nc.tensor.matmul_mx(out=y3[:], lhsT=w3_q[b][0][:, blk(n)].bitcast(FP8X4),
+                                        lhsT_scale=w3_q[b][1][:, blk(n)],
+                                        rhs=xq[b][0][:, half(h)].bitcast(FP8X4), rhs_scale=xq[b][1][:, half(h)],
+                                        start=(b == 0), stop=(b == HP - 1))
+                bounded = buf([P, BANK], F32, "bounded%d" % (n % 2))
+                nc.scalar.activation(out=bounded[:], in_=y4[:], func=ACT.Tanh)
+                result = buf([P, BANK], F32, "habs%d" % n)
+                nc.vector.tensor_tensor(result[:], y3[:], bounded[:], ALU.add)
+                nc.sync.dma_start(out=out[blk(n), half(h)], in_=result[:])

@@ -25,6 +25,7 @@ BANK = 512
 HALF_COLS = BANK // 16
 SLICES = H // P
 LAST = SLICES - 1
+RING = 5
 PAGE_SLOT = [0, 1, 2, 3, 4, 5, 0, 1]
 
 
@@ -87,7 +88,7 @@ def tile_list_bridge_wear_scores_kernel(tc, tab_words, tab_scales, offs, w1, gai
         raw_lo = {}
 
         def load_w1_slice(s):
-            raw = buf([P, KP, 4, P], F32, "raw%d" % (s % 3))
+            raw = buf([P, KP, 4, P], F32, ["raw0", "raw1", "page5", "big2"][s])
             for a in range(KP):
                 rows = w1[a * PASS:(a + 1) * PASS, blk(s)]
                 nc.sync.dma_start(out=raw[:, a, :, :], in_=rows.rearrange("(p j) c -> p j c", j=4))
@@ -105,44 +106,65 @@ def tile_list_bridge_wear_scores_kernel(tc, tab_words, tab_scales, offs, w1, gai
         nc.sync.dma_start(out=rows_lo[4:8, :], in_=amp[0:PASS].rearrange("(s p) -> s p", p=P))
         load_table(1)
         wgs_lo = buf([P, S], F32, "wgs_lo")
-        nc.sync.dma_start(out=wgs_lo[:], in_=wgs)
-        idx2 = load_list(offs2, "idx2")
+        nc.sync.dma_start(out=wgs_lo[:, half(0)], in_=wgs[:, half(0)])
         load_table(2)
+        nc.sync.dma_start(out=wgs_lo[:, half(1)], in_=wgs[:, half(1)])
+        idx2 = load_list(offs2, "idx2")
         load_page(1)
         load_w1_slice(1)
         idx3 = load_list(offs3, "idx3")
-        load_w1_slice(2)
         load_page(2)
+        load_w1_slice(2)
+        gain_hi = buf([P, 4], F32, "gain_hi")
+        nc.sync.dma_start(out=gain_hi[:], in_=gain[PASS:].rearrange("(p t) -> p t", t=4))
+        amp_hi = buf([P, 4], F32, "amp_hi")
+        nc.sync.dma_start(out=amp_hi[:], in_=amp[PASS:].rearrange("(p t) -> p t", t=4))
+        raw_hi = []
+        for a in range(KP):
+            if a == 1:
+                load_page(3)
+                load_w1_slice(3)
+            if a > 0:
+                load_page(3 + a)
+            raw = buf([P, 4, PASS], F32, ["raw0", "raw1", "big2"][a])
+            nc.sync.dma_start(out=raw[:], in_=w1[a * PASS:(a + 1) * PASS, PASS:].rearrange("(p j) c -> p j c", j=4))
+            raw_hi.append(raw)
 
         turned = bank(6)
         nc.tensor.transpose(turned[:, 0:P], rows_lo[:], ident[:])
         cols_lo = buf([P, 8], F32, "cols_lo")
         nc.scalar.copy(out=cols_lo[:], in_=turned[:, 0:8])
         am1_lo = buf([P, 4], F32, "am1_lo")
-        nc.vector.tensor_scalar(out=am1_lo[:], in0=cols_lo[:, 4:8], scalar1=-1.0, scalar2=None, op0=ALU.add)
+        nc.gpsimd.tensor_scalar(out=am1_lo[:], in0=cols_lo[:, 4:8], scalar1=-1.0, scalar2=None, op0=ALU.add)
 
+        am1_hi = buf([P, 3], F32, "am1_hi")
+        nc.gpsimd.tensor_scalar(out=am1_hi[:], in0=amp_hi[:, 0:3], scalar1=-1.0, scalar2=None, op0=ALU.add)
         earlier = {}
         after_page = {}
-        first_two = buf([P, 2 * M], F32, "page4")
+        after_w1 = []
+        first_three = buf([P, 3 * BANK], F32, "first_three")
 
-        def fetch_earlier(s):
-            if s < 2:
-                e = first_two[:, s * M:(s + 1) * M]
+        def fetch_earlier(s, h):
+            if 2 * s + h < 3:
+                e = first_three[:, half(2 * s + h)]
+            elif s == 1:
+                e = after_w1[0][:, half(1)]
+            elif s == 2 or h == 1:
+                e = after_page[s - 2][:, half(h)]
             else:
-                e = after_page[s - 2][:, 0:M]
+                e = buf([P, BANK], F32, "ring%d" % ((s - 3) % RING))[:]
+            looked_up = pages[s][:].indirect(half_list(idx4, h))
             if s == LAST:
-                nc.vector.tensor_copy(out=e, in_=pages[s][:].indirect(idx4[:]))
+                nc.vector.tensor_copy(out=e, in_=looked_up)
             else:
-                for h in range(2):
-                    nc.vector.tensor_scalar(out=e[:, half(h)], in0=pages[s][:].indirect(half_list(idx4, h)),
-                                            scalar1=-1.0, scalar2=0.0, op0=ALU.mult, op1=ALU.add)
-            earlier[s] = e
+                nc.vector.tensor_scalar(out=e, in0=looked_up, scalar1=-1.0, scalar2=0.0, op0=ALU.mult, op1=ALU.add)
+            earlier[s, h] = e
 
         w1_codes = {}
 
         def quantise_w1_slice(s):
             raw = raw_lo[s]
-            grouped = buf([P, KP, P * 4], BF16, ["slot0", "ring0", "slot1", "slot2"][s])
+            grouped = buf([P, KP, P * 4], BF16, ["slot0", "slot1", "ring0", "ring1"][s])
             for a in range(KP):
                 nc.scalar.copy(out=grouped[:, a, :].rearrange("p (c i j) -> p c j i", i=4, j=4),
                                in_=raw[:, a, :, :].rearrange("p j (c i) -> p c j i", i=4))
@@ -152,7 +174,8 @@ def tile_list_bridge_wear_scores_kernel(tc, tab_words, tab_scales, offs, w1, gai
                                   in_=grouped[:].rearrange("p a w -> p (a w)"))
             w1_codes[s] = [(codes[:, blk(a)], scales[:, blk(a)]) for a in range(KP)]
 
-        fetch_earlier(0)
+        fetch_earlier(0, 0)
+        fetch_earlier(0, 1)
         v_sc = buf([P, S], U8, "v_sc")
         nc.vector.tensor_copy(out=v_sc[:], in_=tab_sc[:].indirect(idx[:]))
         v = {}
@@ -168,38 +191,41 @@ def tile_list_bridge_wear_scores_kernel(tc, tab_words, tab_scales, offs, w1, gai
 
         habs = {}
         wg = {}
-        later = {}
+        dealt = {}
+
+        def load_dealt(t):
+            dealt[t] = buf([P, S], F32, ["ring4", "dealt0", "dealt1", "dealt0"][t])
+            rows = wgs.rearrange("(q t) j -> q t j", t=4)[:, t, :]
+            nc.sync.dma_start(out=dealt[t][:], in_=rows.partition_broadcast(4))
 
         def features(s):
             hab = buf([P, S], F32, "habs%d" % (s % 3))
             for h in range(2):
-                acc = bank(h if s == 0 else 2 + h)
-                for a in range(KP):
+                acc = bank(h)
+                for n, a in enumerate(range(KP) if s == 0 else reversed(range(KP))):
                     codes, scales = w1_codes[s][a]
                     nc.tensor.matmul_mx(out=acc[:], lhsT=codes.bitcast(FP8X4), lhsT_scale=scales,
                                         rhs=v[a][:, half(h)].bitcast(FP8X4), rhs_scale=v_sc[4 * a:P, half(h)],
-                                        start=(a == 0), stop=(a == KP - 1))
+                                        start=(n == 0), stop=(n == KP - 1))
                 nc.scalar.activation(out=hab[:, half(h)], in_=acc[:], func=ACT.Abs)
             habs[s] = hab
 
         def gained_weights(s):
-            w = buf([P, S], F32, "wg0")[:] if s == 0 else after_page[s - 1][:, M:]
+            w = after_page[s - 1][:, M:]
             if s < 4:
                 nc.scalar.activation(out=w, in_=wgs_lo[:], func=ACT.Copy, scale=cols_lo[:, s:s + 1])
             else:
-                nc.scalar.activation(out=w, in_=later["wgs"][:, s - 4, :], func=ACT.Copy,
-                                     scale=later["gain"][:, s - 4:s - 3])
+                nc.scalar.activation(out=w, in_=dealt[s - 4][:], func=ACT.Copy, scale=gain_hi[:, s - 4:s - 3])
             wg[s] = w
 
-        def put(s):
-            if s == 0:
-                for h in range(2):
-                    nc.vector.tensor_tensor(pages[s][:].indirect(half_list(idx2, h)), habs[s][:, half(h)],
-                                            wg[s][:, half(h)], ALU.mult)
-            else:
-                nc.vector.tensor_tensor(pages[s][:].indirect(idx2[:]), habs[s][:], wg[s], ALU.mult)
+        def put_first(h, w):
+            nc.scalar.activation(out=w, in_=wgs_lo[:, half(h)], func=ACT.Copy, scale=cols_lo[:, 0:1])
+            nc.vector.tensor_tensor(pages[0][:].indirect(half_list(idx2, h)), habs[0][:, half(h)], w, ALU.mult)
 
-        xq = [(buf([P, M], U32, "xq%d" % b), buf([P, M], U8, "xs%d" % b)) for b in range(HP)]
+        def put(s):
+            nc.vector.tensor_tensor(pages[s][:].indirect(idx2[:]), habs[s][:], wg[s], ALU.mult)
+
+        xq = {1: (buf([P, M], U32, "xq1"), buf([P, M], U8, "xs1"))}
         planes = [buf([P, 4, BANK], BF16, "plane%d" % h) for h in range(2)]
         turned_parts = {}
 
@@ -214,22 +240,32 @@ def tile_list_bridge_wear_scores_kernel(tc, tab_words, tab_scales, offs, w1, gai
         changed = {}
 
         def fetch_changed(s):
-            c = buf([P, M], F32, "ring%d" % (s % 2))
+            c = buf([P, M], F32, "ring%d" % (s % RING))
             nc.vector.tensor_copy(out=c[:], in_=pages[s][:].indirect(idx3[:]))
             changed[s] = c
-            after_page[s] = buf([P, T2], F32, "page%d" % PAGE_SLOT[s])
+            if s < LAST:
+                after_page[s] = buf([P, T2], F32, "page%d" % PAGE_SLOT[s])
+
+        linear = {}
+
+        def scale_changed(s):
+            lin = buf([P, M], F32, "ring%d" % ((s + 1) % RING))
+            am1 = am1_lo[:, s:s + 1] if s < 4 else am1_hi[:, s - 4:s - 3]
+            for h in range(2):
+                nc.scalar.activation(out=lin[:, half(h)], in_=changed[s][:, half(h)], func=ACT.Copy, scale=am1)
+            linear[s] = lin
 
         def compare(s):
             c = changed[s]
-            lin = buf([P, M], F32, "ring%d" % ((s + 1) % 2))
-            am1 = am1_lo[:, s:s + 1] if s < 4 else later["am1"][:, s - 4:s - 3]
+            lin = linear[s]
             if s == 0:
                 turned_parts["over"] = buf([P, 8, 4, P], F32, "big0")
                 turned_parts["lin"] = buf([P, 8, 4, P], F32, "big1")
             if s >= 4:
-                turned_parts["over"] = buf([P, M], F32, "big0")
-                turned_parts["lin"] = buf([P, M], F32, "big1")
-            over_t, lin_t = turned_parts["over"], turned_parts["lin"]
+                both = buf([P, 2, M], F32, "big2")
+                over_t, lin_t = both[:, 0, :], both[:, 1, :]
+            else:
+                over_t, lin_t = turned_parts["over"], turned_parts["lin"]
 
             def leave(dst, h, src, func):
                 if s < 4:
@@ -239,92 +275,81 @@ def tile_list_bridge_wear_scores_kernel(tc, tab_words, tab_scales, offs, w1, gai
                     nc.scalar.activation(out=dst[:, half(h)], in_=src[:], func=func)
 
             for h in range(2):
-                nc.scalar.activation(out=lin[:, half(h)], in_=c[:, half(h)], func=ACT.Copy, scale=am1)
-            for h in range(2):
                 diff = bank(2 + h)
                 for i in range(4):
-                    add_turned(diff[:, blk(i)], earlier[s][:, blk(4 * h + i)], c[:, blk(4 * h + i)])
+                    add_turned(diff[:, blk(i)], c[:, blk(4 * h + i)], earlier[s, h][:, blk(i)])
                 leave(over_t, h, diff, ACT.Relu)
                 lin_bank = bank(4 + h)
                 for i in range(4):
                     nc.tensor.transpose(lin_bank[:, blk(i)], lin[:, blk(4 * h + i)], ident[:])
                 leave(lin_t, h, lin_bank, ACT.Copy)
                 if s >= 4:
-                    back = bank(6 + h)
+                    back = bank((0 if s == 5 else 6) + h)
                     for i in range(4):
                         add_turned(back[:, blk(i)], over_t[:, blk(4 * h + i)], lin_t[:, blk(4 * h + i)])
                     nc.scalar.copy(out=planes[h][:, s - 4, :], in_=back[:])
 
-        def first_block_back():
-            over_t, lin_t = turned_parts["over"], turned_parts["lin"]
-            for h in range(2):
-                grouped = buf([P, BANK, 4], BF16, "slot%d" % [1, 3][h])
-                for i in range(4):
-                    mb = 4 * h + i
-                    back = bank([0, 1, 6, 7][i])
-                    for t in range(4):
-                        add_turned(back[:, blk(t)], over_t[:, mb, t, :], lin_t[:, mb, t, :])
-                    nc.scalar.copy(out=grouped[:, blk(i), :], in_=back[:].rearrange("p (t m) -> p m t", t=4))
-                quantise_x(0, h, grouped)
+        first_x = {}
 
-        def compare_last(h):
+        def first_block_back(blocks, first_bank):
+            over_t, lin_t = turned_parts["over"], turned_parts["lin"]
+            for mb in blocks:
+                h, i = divmod(mb, 4)
+                if i == 0:
+                    first_x[h] = buf([P, BANK, 4], BF16, "slot%d" % h)
+                back = bank(first_bank + mb % 2)
+                for t in range(4):
+                    add_turned(back[:, blk(t)], over_t[:, mb, t, :], lin_t[:, mb, t, :])
+                nc.scalar.copy(out=first_x[h][:, blk(i), :], in_=back[:].rearrange("p (t m) -> p m t", t=4))
+
+        def compare_last(h, last_changed):
             s = LAST
-            c = buf([P, BANK], F32, ["ring1", "low0"][h])
-            nc.vector.tensor_copy(out=c[:], in_=pages[s][:].indirect(half_list(idx3, h)))
-            low = buf([P, BANK], F32, ["low0", "low1"][h])
-            nc.vector.tensor_tensor(low[:], c[:], earlier[s][:, half(h)], ALU.min)
-            nc.vector.scalar_tensor_tensor(out=planes[h][:, 3, :], in0=c[:], scalar=later["amp"][:, 3:4], in1=low[:],
+            c = last_changed[:, half(h)]
+            nc.vector.tensor_copy(out=c, in_=pages[s][:].indirect(half_list(idx3, h)))
+            low = buf([P, BANK], F32, "raw%d" % h)
+            nc.vector.tensor_tensor(low[:], c, earlier[s, h], ALU.min)
+            nc.vector.scalar_tensor_tensor(out=planes[h][:, 3, :], in0=c, scalar=amp_hi[:, 3:4], in1=low[:],
                                            op0=ALU.mult, op1=ALU.subtract)
-            grouped = buf([P, BANK, 4], BF16, "slot0")
-            weave = nc.scalar.copy if h == 0 else nc.vector.tensor_copy
+            grouped = buf([P, BANK, 4], BF16, ["slot1", "slot2"][h])
+            weave = nc.scalar.copy if h == 1 else nc.vector.tensor_copy
             weave(out=grouped[:].rearrange("p (c i) t -> p c t i", i=4),
                   in_=planes[h][:].rearrange("p t (c i) -> p c t i", i=4))
-            quantise_x(1, h, grouped)
+            return grouped
 
-        def second_block_weights():
-            gain_hi = buf([P, 4], F32, "gain_hi")
-            nc.sync.dma_start(out=gain_hi[:], in_=gain[PASS:].rearrange("(p t) -> p t", t=4))
-            amp_hi = buf([P, 4], F32, "amp_hi")
-            nc.sync.dma_start(out=amp_hi[:], in_=amp[PASS:].rearrange("(p t) -> p t", t=4))
-            am1_hi = buf([P, 3], F32, "am1_hi")
-            nc.vector.tensor_scalar(out=am1_hi[:], in0=amp_hi[:, 0:3], scalar1=-1.0, scalar2=None, op0=ALU.add)
-            passes = []
-            for a in range(KP):
-                raw = buf([P, 4, PASS], F32, "raw%d" % ((a + 1) % 3))
-                rows = w1[a * PASS:(a + 1) * PASS, PASS:]
-                nc.sync.dma_start(out=raw[:], in_=rows.rearrange("(p j) c -> p j c", j=4))
-                grouped = buf([P, PASS * 4], BF16, "slot%d" % [0, 1, 3][a])
-                nc.scalar.copy(out=grouped[:].rearrange("p (t m j) -> p m j t", t=4, j=4),
-                               in_=raw[:].rearrange("p j (m t) -> p m j t", t=4))
-                codes = buf([P, PASS], U32, "w1hc%d" % a)
-                scales = buf([P, PASS], U8, "w1hs%d" % a)
-                nc.vector.quantize_mx(out=codes[:].bitcast(FP8X4), scales=scales[:], in_=grouped[:])
-                passes.append((codes, scales))
-            for t in range(4):
-                w1_codes[4 + t] = [(codes[:, blk(t)], scales[:, blk(t)]) for codes, scales in passes]
-            load_page(3)
-            dealt = buf([P, 4, S], F32, "big2")
+        hi_passes = []
+
+        def quantise_w1_hi(a):
+            grouped = buf([P, PASS * 4], BF16, ["slot0", "slot2", "ring2"][a])
             for g in range(4):
-                nc.sync.dma_start(out=dealt[32 * g:32 * g + 32, :, :], in_=wgs.rearrange("(q t) j -> q t j", t=4))
-            later["gain"] = gain_hi
-            later["amp"] = amp_hi
-            later["am1"] = am1_hi
-            later["wgs"] = dealt
+                nc.scalar.copy(out=grouped[:].rearrange("p (t m j) -> p m j t", t=4, j=4)[:, 32 * g:32 * g + 32, :, :],
+                               in_=raw_hi[a][:].rearrange("p j (m t) -> p m j t", t=4)[:, 32 * g:32 * g + 32, :, :])
+            codes = buf([P, PASS], U32, "w1hc%d" % a)
+            scales = buf([P, PASS], U8, "w1hs%d" % a)
+            nc.vector.quantize_mx(out=codes[:].bitcast(FP8X4), scales=scales[:], in_=grouped[:])
+            hi_passes.append((codes, scales))
+            if a == KP - 1:
+                for t in range(4):
+                    w1_codes[4 + t] = [(c[:, blk(t)], sc[:, blk(t)]) for c, sc in hi_passes]
 
         w3_q = []
         w4_w = []
 
-        def second_stage_weights():
+        def quantise_w3():
+            both = buf([P, HP, N * 4], BF16, "ring3")
+            all_codes = buf([P, HP * N], U32, "w3c")
             for b in range(HP):
-                raw = buf([P, 4, N], F32, "raw%d" % (b + 1))
+                raw = buf([P, 4, N], F32, "raw%d" % b)
                 nc.sync.dma_start(out=raw[:], in_=w3[b * PASS:(b + 1) * PASS, :].rearrange("(p j) n -> p j n", j=4))
-                grouped = buf([P, N * 4], BF16, "slot%d" % [2, 0][b])
-                nc.scalar.copy(out=grouped[:].rearrange("p (c i j) -> p c j i", i=4, j=4),
-                               in_=raw[:].rearrange("p j (c i) -> p c j i", i=4))
-                codes = buf([P, N], U32, "w3c%d" % b)
+                for g in range(3):
+                    nc.scalar.copy(out=both[:, b, :].rearrange("p (c i j) -> p c j i", i=4, j=4)[:, 32 * g:32 * g + 32, :, :],
+                                   in_=raw[:].rearrange("p j (c i) -> p c j i", i=4)[:, 32 * g:32 * g + 32, :, :])
+                codes = all_codes[:, b * N:(b + 1) * N]
                 scales = buf([P, N], U8, "w3s%d" % b)
-                nc.vector.quantize_mx(out=codes[:].bitcast(FP8X4), scales=scales[:], in_=grouped[:])
+                nc.vector.quantize_mx(out=codes.bitcast(FP8X4), scales=scales[:], in_=both[:, b, :])
                 w3_q.append((codes, scales))
+
+        def load_w4():
+            for b in range(HP):
                 words = buf([P, 2 * N], U8, "w4w%d" % b)
                 nc.sync.dma_start(out=words[:].bitcast(I32), in_=w4_words[b].bitcast(I32))
                 w4_w.append(words)
@@ -332,39 +357,65 @@ def tile_list_bridge_wear_scores_kernel(tc, tab_words, tab_scales, offs, w1, gai
                 nc.sync.dma_start(out=w4_sc[32 * q:32 * q + 4, :].bitcast(I32).rearrange("r (b n) -> r b n", b=HP),
                                   in_=w4_scales[:, 4 * q:4 * q + 4, :].bitcast(I32).rearrange("b r n -> r b n"))
 
-        gained_weights(0)
         features(0)
-        fetch_earlier(1)
+        put_first(0, buf([P, BANK], F32, "wg0")[:])
+        fetch_earlier(1, 0)
         quantise_w1_slice(1)
+        after_w1.append(buf([P, M], F32, "slot1"))
+        fetch_earlier(1, 1)
+        put_first(1, after_w1[0][:, half(0)])
         features(1)
         quantise_w1_slice(2)
-        load_w1_slice(3)
-        quantise_w1_slice(3)
-        second_block_weights()
-        load_page(5)
+        features(2)
+        load_dealt(0)
+        load_dealt(1)
         for s in range(SLICES):
-            put(s)
+            if s > 0:
+                put(s)
             if s == LAST:
                 break
+            if 1 <= s < SLICES - 2:
+                fetch_earlier(s + 2, 0)
             fetch_changed(s)
             gained_weights(s + 1)
+            if s in (4, 5):
+                first_block_back(range(3 * s - 10, 3 * s - 7), 4)
+            scale_changed(s)
+            if s == 0:
+                fetch_earlier(2, 0)
             if s + 2 < SLICES:
-                fetch_earlier(s + 2)
+                fetch_earlier(s + 2, 1)
             compare(s)
-            if s + 2 < SLICES:
-                features(s + 2)
-            if s == 3:
-                first_block_back()
+            if s == 0:
+                quantise_w1_hi(0)
+                quantise_w1_slice(3)
+            if s == 0:
+                quantise_w1_hi(1)
             if s == 1:
-                load_page(4)
+                quantise_w1_hi(2)
             if s in (2, 3):
                 load_page(s + 4)
             if s == 2:
-                second_stage_weights()
+                quantise_w3()
+            if s in (3, 4):
+                load_dealt(s - 1)
+            for ahead in [[3], [4], [5], [6], [7], [], []][s]:
+                features(ahead)
+            if s == 3:
+                first_block_back(range(2), 2)
+            if s == 5:
+                xq[0] = (buf([P, M], U32, "ring%d" % (s % RING)), buf([P, M], U8, "xs0"))
+                for h in range(2):
+                    quantise_x(0, h, first_x[h])
+                load_w4()
 
+        all_bounded = buf([P, 6 * BANK], F32, "big0")
+        all_results = buf([P, 6 * BANK], F32, "big1")
         order = [0, 1, 2, 3, 4, 5, 6, 7, 0, 1, 2, 3]
+        last_changed = buf([P, M], F32, "ring%d" % (LAST % RING))
+        last_x = {h: compare_last(h, last_changed) for h in (1, 0)}
         for h in range(2):
-            compare_last(h)
+            quantise_x(1, h, last_x[h])
         for h in range(2):
             for n in range(N // P):
                 g = 2 * (h * (N // P) + n)
@@ -380,8 +431,8 @@ def tile_list_bridge_wear_scores_kernel(tc, tab_words, tab_scales, offs, w1, gai
                                         lhsT_scale=w3_q[b][1][:, blk(n)],
                                         rhs=xq[b][0][:, half(h)].bitcast(FP8X4), rhs_scale=xq[b][1][:, half(h)],
                                         start=(b == 0), stop=(b == HP - 1))
-                bounded = buf([P, BANK], F32, "bounded%d" % (n % 2))
-                nc.scalar.activation(out=bounded[:], in_=y4[:], func=ACT.Tanh)
-                result = buf([P, BANK], F32, "habs%d" % n)
-                nc.vector.tensor_tensor(result[:], y3[:], bounded[:], ALU.add)
-                nc.sync.dma_start(out=out[blk(n), half(h)], in_=result[:])
+                bounded = all_bounded[:, half(g // 2)]
+                nc.scalar.activation(out=bounded, in_=y4[:], func=ACT.Tanh)
+                result = all_results[:, half(g // 2)]
+                nc.vector.tensor_tensor(result, y3[:], bounded, ALU.add)
+                nc.sync.dma_start(out=out[blk(n), half(h)], in_=result)

@@ -88,7 +88,7 @@ def tile_list_bridge_wear_scores_kernel(tc, tab_words, tab_scales, offs, w1, gai
         raw_lo = {}
 
         def load_w1_slice(s):
-            raw = buf([P, KP, 4, P], F32, ["raw0", "raw1", "page5", "big2"][s])
+            raw = buf([P, KP, 4, P], F32, ["raw0", "raw1", "page5", "raw2"][s])
             for a in range(KP):
                 rows = w1[a * PASS:(a + 1) * PASS, blk(s)]
                 nc.sync.dma_start(out=raw[:, a, :, :], in_=rows.rearrange("(p j) c -> p j c", j=4))
@@ -102,9 +102,9 @@ def tile_list_bridge_wear_scores_kernel(tc, tab_words, tab_scales, offs, w1, gai
         load_table(0)
         idx = load_list(offs, "idx")
         load_w1_slice(0)
+        load_table(1)
         nc.sync.dma_start(out=rows_lo[0:4, :], in_=gain[0:PASS].rearrange("(s p) -> s p", p=P))
         nc.sync.dma_start(out=rows_lo[4:8, :], in_=amp[0:PASS].rearrange("(s p) -> s p", p=P))
-        load_table(1)
         wgs_lo = buf([P, S], F32, "wgs_lo")
         nc.sync.dma_start(out=wgs_lo[:, half(0)], in_=wgs[:, half(0)])
         load_table(2)
@@ -124,11 +124,11 @@ def tile_list_bridge_wear_scores_kernel(tc, tab_words, tab_scales, offs, w1, gai
             if a == 1:
                 load_page(3)
                 load_w1_slice(3)
-            if a > 0:
-                load_page(3 + a)
+                load_page(4)
             raw = buf([P, 4, PASS], F32, ["raw0", "raw1", "big2"][a])
             nc.sync.dma_start(out=raw[:], in_=w1[a * PASS:(a + 1) * PASS, PASS:].rearrange("(p j) c -> p j c", j=4))
             raw_hi.append(raw)
+        load_page(5)
 
         turned = bank(6)
         nc.tensor.transpose(turned[:, 0:P], rows_lo[:], ident[:])
@@ -164,7 +164,7 @@ def tile_list_bridge_wear_scores_kernel(tc, tab_words, tab_scales, offs, w1, gai
 
         def quantise_w1_slice(s):
             raw = raw_lo[s]
-            grouped = buf([P, KP, P * 4], BF16, ["slot0", "slot1", "ring0", "ring1"][s])
+            grouped = buf([P, KP, P * 4], BF16, ["slot2", "slot1", "ring0", "ring1"][s])
             for a in range(KP):
                 nc.scalar.copy(out=grouped[:, a, :].rearrange("p (c i j) -> p c j i", i=4, j=4),
                                in_=raw[:, a, :, :].rearrange("p j (c i) -> p c j i", i=4))
@@ -201,7 +201,7 @@ def tile_list_bridge_wear_scores_kernel(tc, tab_words, tab_scales, offs, w1, gai
         def features(s):
             hab = buf([P, S], F32, "habs%d" % (s % 3))
             for h in range(2):
-                acc = bank(h)
+                acc = bank(h if s in (0, 2) else 2 + h)
                 for n, a in enumerate(range(KP) if s == 0 else reversed(range(KP))):
                     codes, scales = w1_codes[s][a]
                     nc.tensor.matmul_mx(out=acc[:], lhsT=codes.bitcast(FP8X4), lhsT_scale=scales,
@@ -225,12 +225,12 @@ def tile_list_bridge_wear_scores_kernel(tc, tab_words, tab_scales, offs, w1, gai
         def put(s):
             nc.vector.tensor_tensor(pages[s][:].indirect(idx2[:]), habs[s][:], wg[s], ALU.mult)
 
-        xq = {1: (buf([P, M], U32, "xq1"), buf([P, M], U8, "xs1"))}
+        xq = [(buf([P, M], U32, "xq%d" % b), buf([P, M], U8, "xs%d" % b)) for b in range(HP)]
         planes = [buf([P, 4, BANK], BF16, "plane%d" % h) for h in range(2)]
         turned_parts = {}
 
-        def quantise_x(b, h, grouped):
-            nc.vector.quantize_mx(out=xq[b][0][:, half(h)].bitcast(FP8X4), scales=xq[b][1][:, half(h)],
+        def quantise_x(b, cols, grouped):
+            nc.vector.quantize_mx(out=xq[b][0][:, cols].bitcast(FP8X4), scales=xq[b][1][:, cols],
                                   in_=grouped[:].rearrange("p m t -> p (m t)"))
 
         def add_turned(dst, first, second):
@@ -283,24 +283,28 @@ def tile_list_bridge_wear_scores_kernel(tc, tab_words, tab_scales, offs, w1, gai
                 for i in range(4):
                     nc.tensor.transpose(lin_bank[:, blk(i)], lin[:, blk(4 * h + i)], ident[:])
                 leave(lin_t, h, lin_bank, ACT.Copy)
-                if s >= 4:
-                    back = bank((0 if s == 5 else 6) + h)
+            if s == 3:
+                first_block_back([0, 1], [6, 7], "ring4")
+            if s == 4:
+                first_block_back([2, 3, 4], [0, 1, 6], "ring0")
+            if s == 5:
+                first_block_back([5, 6, 7], [6, 7, 1], "ring1")
+            if s >= 4:
+                for h in range(2):
+                    back = bank({4: [7, 0], 5: [0, 1], 6: [6, 7]}[s][h])
                     for i in range(4):
                         add_turned(back[:, blk(i)], over_t[:, blk(4 * h + i)], lin_t[:, blk(4 * h + i)])
                     nc.scalar.copy(out=planes[h][:, s - 4, :], in_=back[:])
 
-        first_x = {}
-
-        def first_block_back(blocks, first_bank):
+        def first_block_back(blocks, banks, tag):
             over_t, lin_t = turned_parts["over"], turned_parts["lin"]
-            for mb in blocks:
-                h, i = divmod(mb, 4)
-                if i == 0:
-                    first_x[h] = buf([P, BANK, 4], BF16, "slot%d" % h)
-                back = bank(first_bank + mb % 2)
+            grouped = buf([P, len(blocks) * P, 4], BF16, tag)
+            for i, mb in enumerate(blocks):
+                back = bank(banks[i % len(banks)])
                 for t in range(4):
                     add_turned(back[:, blk(t)], over_t[:, mb, t, :], lin_t[:, mb, t, :])
-                nc.scalar.copy(out=first_x[h][:, blk(i), :], in_=back[:].rearrange("p (t m) -> p m t", t=4))
+                nc.scalar.copy(out=grouped[:, blk(i), :], in_=back[:].rearrange("p (t m) -> p m t", t=4))
+            quantise_x(0, slice(blocks[0] * P, (blocks[-1] + 1) * P), grouped)
 
         def compare_last(h, last_changed):
             s = LAST
@@ -319,7 +323,7 @@ def tile_list_bridge_wear_scores_kernel(tc, tab_words, tab_scales, offs, w1, gai
         hi_passes = []
 
         def quantise_w1_hi(a):
-            grouped = buf([P, PASS * 4], BF16, ["slot0", "slot2", "ring2"][a])
+            grouped = buf([P, PASS * 4], BF16, ["slot2", "slot2", "ring2"][a])
             for g in range(4):
                 nc.scalar.copy(out=grouped[:].rearrange("p (t m j) -> p m j t", t=4, j=4)[:, 32 * g:32 * g + 32, :, :],
                                in_=raw_hi[a][:].rearrange("p j (m t) -> p m j t", t=4)[:, 32 * g:32 * g + 32, :, :])
@@ -348,11 +352,13 @@ def tile_list_bridge_wear_scores_kernel(tc, tab_words, tab_scales, offs, w1, gai
                 nc.vector.quantize_mx(out=codes.bitcast(FP8X4), scales=scales[:], in_=both[:, b, :])
                 w3_q.append((codes, scales))
 
-        def load_w4():
+        def load_w4_words():
+            words = buf([P, HP * 2 * N], U8, "page%d" % PAGE_SLOT[LAST])
             for b in range(HP):
-                words = buf([P, 2 * N], U8, "w4w%d" % b)
-                nc.sync.dma_start(out=words[:].bitcast(I32), in_=w4_words[b].bitcast(I32))
-                w4_w.append(words)
+                w4_w.append(words[:, b * 2 * N:(b + 1) * 2 * N])
+                nc.sync.dma_start(out=w4_w[b].bitcast(I32), in_=w4_words[b].bitcast(I32))
+
+        def load_w4_scales():
             for q in range(4):
                 nc.sync.dma_start(out=w4_sc[32 * q:32 * q + 4, :].bitcast(I32).rearrange("r (b n) -> r b n", b=HP),
                                   in_=w4_scales[:, 4 * q:4 * q + 4, :].bitcast(I32).rearrange("b r n -> r b n"))
@@ -378,8 +384,6 @@ def tile_list_bridge_wear_scores_kernel(tc, tab_words, tab_scales, offs, w1, gai
                 fetch_earlier(s + 2, 0)
             fetch_changed(s)
             gained_weights(s + 1)
-            if s in (4, 5):
-                first_block_back(range(3 * s - 10, 3 * s - 7), 4)
             scale_changed(s)
             if s == 0:
                 fetch_earlier(2, 0)
@@ -389,9 +393,8 @@ def tile_list_bridge_wear_scores_kernel(tc, tab_words, tab_scales, offs, w1, gai
             if s == 0:
                 quantise_w1_hi(0)
                 quantise_w1_slice(3)
-            if s == 0:
-                quantise_w1_hi(1)
             if s == 1:
+                quantise_w1_hi(1)
                 quantise_w1_hi(2)
             if s in (2, 3):
                 load_page(s + 4)
@@ -399,23 +402,19 @@ def tile_list_bridge_wear_scores_kernel(tc, tab_words, tab_scales, offs, w1, gai
                 quantise_w3()
             if s in (3, 4):
                 load_dealt(s - 1)
-            for ahead in [[3], [4], [5], [6], [7], [], []][s]:
+            for ahead in [[], [3], [4, 5], [6], [7], [], []][s]:
                 features(ahead)
-            if s == 3:
-                first_block_back(range(2), 2)
             if s == 5:
-                xq[0] = (buf([P, M], U32, "ring%d" % (s % RING)), buf([P, M], U8, "xs0"))
-                for h in range(2):
-                    quantise_x(0, h, first_x[h])
-                load_w4()
+                load_w4_scales()
 
         all_bounded = buf([P, 6 * BANK], F32, "big0")
         all_results = buf([P, 6 * BANK], F32, "big1")
         order = [0, 1, 2, 3, 4, 5, 6, 7, 0, 1, 2, 3]
         last_changed = buf([P, M], F32, "ring%d" % (LAST % RING))
         last_x = {h: compare_last(h, last_changed) for h in (1, 0)}
+        load_w4_words()
         for h in range(2):
-            quantise_x(1, h, last_x[h])
+            quantise_x(1, half(h), last_x[h])
         for h in range(2):
             for n in range(N // P):
                 g = 2 * (h * (N // P) + n)

@@ -18,15 +18,22 @@ ALU = mybir.AluOpType
 ACT = mybir.ActivationFunctionType
 
 P = 128
-PASS = 512
-KP = K // PASS
-HP = H // PASS
+PACK = 4
+PASS = P * PACK
+K_PASSES = K // PASS
+R_PASSES = H // PASS
 BANK = 512
-HALF_COLS = BANK // 16
+QUADS = 4
 SLICES = H // P
 LAST = SLICES - 1
+PAGE_BUFFERS = 6
+FEATURE_BUFFERS = 3
 RING = 5
-PAGE_SLOT = [0, 1, 2, 3, 4, 5, 0, 1]
+SPARE_BANKS = 0
+DIFF_BANKS = 2
+LINEAR_BANKS = 4
+BACK_BANKS = 6
+FEATURE_BANKS = [SPARE_BANKS, DIFF_BANKS, SPARE_BANKS, SPARE_BANKS, SPARE_BANKS, DIFF_BANKS, BACK_BANKS, DIFF_BANKS]
 
 
 def tile_list_bridge_wear_scores_kernel(tc, tab_words, tab_scales, offs, w1, gain, page0, wgs,
@@ -40,6 +47,12 @@ def tile_list_bridge_wear_scores_kernel(tc, tab_words, tab_scales, offs, w1, gai
         def buf(shape, dtype, tag):
             return sb.tile(shape, dtype, tag=tag, name=tag, align_bytes=64)
 
+        def ring(i):
+            return "ring%d" % (i % RING)
+
+        def page_buffer(s):
+            return "page%d" % (s % PAGE_BUFFERS)
+
         def bank(b):
             return ps.tile([P, BANK], F32, tag="bank%d" % b, name="bank%d" % b)
 
@@ -52,7 +65,7 @@ def tile_list_bridge_wear_scores_kernel(tc, tab_words, tab_scales, offs, w1, gai
             return slice(h * BANK, (h + 1) * BANK)
 
         def half_list(entries, h):
-            return entries[:, h * HALF_COLS:(h + 1) * HALF_COLS]
+            return entries[:, h * (BANK // 16):(h + 1) * (BANK // 16)]
 
         def blk(i):
             return slice(i * P, (i + 1) * P)
@@ -61,20 +74,20 @@ def tile_list_bridge_wear_scores_kernel(tc, tab_words, tab_scales, offs, w1, gai
         make_identity(nc, ident[:])
         tab_sc = buf([P, T], U8, "tab_sc")
         nc.vector.memset(tab_sc[:].bitcast(I32), 0)
-        rows_lo = buf([P, P], F32, "rows_lo")
-        nc.vector.memset(rows_lo[:], 0.0)
-        w4_sc = buf([P, HP * N], U8, "w4_sc")
+        factor_rows = buf([P, P], F32, "factor_rows")
+        nc.vector.memset(factor_rows[:], 0.0)
+        w4_sc = buf([P, R_PASSES * N], U8, "w4_sc")
         nc.vector.memset(w4_sc[:].bitcast(I32), 0)
 
         pages = {}
 
         def load_page(s):
-            page = buf([P, T2], F32, "page%d" % PAGE_SLOT[s])
-            if s < 4:
-                src = page0[blk(s), :]
+            page = buf([P, T2], F32, page_buffer(s))
+            if s < PACK:
+                rows = page0[blk(s), :]
             else:
-                src = page0[PASS:, :].rearrange("(p t) c -> p t c", t=4)[:, s - 4, :]
-            nc.sync.dma_start(out=page[:], in_=src)
+                rows = page0[PASS:, :].rearrange("(p t) c -> p t c", t=PACK)[:, s - PACK, :]
+            nc.sync.dma_start(out=page[:], in_=rows)
             pages[s] = page
 
         tab = {}
@@ -85,353 +98,336 @@ def tile_list_bridge_wear_scores_kernel(tc, tab_words, tab_scales, offs, w1, gai
                               in_=tab_words[a].rearrange("p t i -> p (t i)").bitcast(I32))
             tab[a] = words
 
-        raw_lo = {}
+        w1_slice_raw = {}
 
-        def load_w1_slice(s):
-            raw = buf([P, KP, 4, P], F32, ["raw0", "raw1", "page5", "raw2"][s])
-            for a in range(KP):
+        def load_w1_slice(s, tag):
+            raw = buf([P, K_PASSES, PACK, P], F32, tag)
+            for a in range(K_PASSES):
                 rows = w1[a * PASS:(a + 1) * PASS, blk(s)]
-                nc.sync.dma_start(out=raw[:, a, :, :], in_=rows.rearrange("(p j) c -> p j c", j=4))
-            raw_lo[s] = raw
+                nc.sync.dma_start(out=raw[:, a, :, :], in_=rows.rearrange("(p j) c -> p j c", j=PACK))
+            w1_slice_raw[s] = raw
+
+        def load_pass(weight, a, cols, tag):
+            raw = buf([P, PACK, cols.stop - cols.start], F32, tag)
+            nc.sync.dma_start(out=raw[:], in_=weight[a * PASS:(a + 1) * PASS, cols].rearrange("(p j) c -> p j c", j=PACK))
+            return raw
 
         load_page(0)
         idx4 = load_list(offs4, "idx4")
-        for q in range(4):
-            nc.sync.dma_start(out=tab_sc[32 * q:32 * q + 4 * KP, :].bitcast(I32),
+        for q in range(QUADS):
+            nc.sync.dma_start(out=tab_sc[32 * q:32 * q + 4 * K_PASSES, :].bitcast(I32),
                               in_=tab_scales[:, 4 * q:4 * q + 4, :].bitcast(I32))
         load_table(0)
         idx = load_list(offs, "idx")
-        load_w1_slice(0)
+        load_w1_slice(0, "raw0")
         load_table(1)
-        nc.sync.dma_start(out=rows_lo[0:4, :], in_=gain[0:PASS].rearrange("(s p) -> s p", p=P))
-        nc.sync.dma_start(out=rows_lo[4:8, :], in_=amp[0:PASS].rearrange("(s p) -> s p", p=P))
-        wgs_lo = buf([P, S], F32, "wgs_lo")
-        nc.sync.dma_start(out=wgs_lo[:, half(0)], in_=wgs[:, half(0)])
+        nc.sync.dma_start(out=factor_rows[0:PACK, :], in_=gain[0:PASS].rearrange("(s p) -> s p", p=P))
+        nc.sync.dma_start(out=factor_rows[PACK:2 * PACK, :], in_=amp[0:PASS].rearrange("(s p) -> s p", p=P))
+        wgs_first = buf([P, S], F32, "wgs_first")
+        nc.sync.dma_start(out=wgs_first[:, half(0)], in_=wgs[:, half(0)])
         load_table(2)
-        nc.sync.dma_start(out=wgs_lo[:, half(1)], in_=wgs[:, half(1)])
+        nc.sync.dma_start(out=wgs_first[:, half(1)], in_=wgs[:, half(1)])
         idx2 = load_list(offs2, "idx2")
         load_page(1)
-        load_w1_slice(1)
+        load_w1_slice(1, "raw1")
         idx3 = load_list(offs3, "idx3")
         load_page(2)
-        load_w1_slice(2)
-        gain_hi = buf([P, 4], F32, "gain_hi")
-        nc.sync.dma_start(out=gain_hi[:], in_=gain[PASS:].rearrange("(p t) -> p t", t=4))
-        amp_hi = buf([P, 4], F32, "amp_hi")
-        nc.sync.dma_start(out=amp_hi[:], in_=amp[PASS:].rearrange("(p t) -> p t", t=4))
-        raw_hi = []
-        for a in range(KP):
-            if a == 1:
-                load_page(3)
-                load_w1_slice(3)
-                load_page(4)
-            raw = buf([P, 4, PASS], F32, ["raw0", "raw1", "big2"][a])
-            nc.sync.dma_start(out=raw[:], in_=w1[a * PASS:(a + 1) * PASS, PASS:].rearrange("(p j) c -> p j c", j=4))
-            raw_hi.append(raw)
+        load_w1_slice(2, page_buffer(5))
+        gain_second = buf([P, PACK], F32, "gain_second")
+        nc.sync.dma_start(out=gain_second[:], in_=gain[PASS:].rearrange("(p t) -> p t", t=PACK))
+        amp_second = buf([P, PACK], F32, "amp_second")
+        nc.sync.dma_start(out=amp_second[:], in_=amp[PASS:].rearrange("(p t) -> p t", t=PACK))
+        second_columns = slice(PASS, H)
+        w1_second_raw = [load_pass(w1, 0, second_columns, "raw0")]
+        load_page(3)
+        load_w1_slice(3, "raw2")
+        load_page(4)
+        w1_second_raw.append(load_pass(w1, 1, second_columns, "raw1"))
+        w1_second_raw.append(load_pass(w1, 2, second_columns, "big2"))
         load_page(5)
+        w3_raw = [load_pass(w3, 0, slice(0, N), "raw2"), load_pass(w3, 1, slice(0, N), "raw0")]
 
-        turned = bank(6)
-        nc.tensor.transpose(turned[:, 0:P], rows_lo[:], ident[:])
-        cols_lo = buf([P, 8], F32, "cols_lo")
-        nc.scalar.copy(out=cols_lo[:], in_=turned[:, 0:8])
-        am1_lo = buf([P, 4], F32, "am1_lo")
-        nc.gpsimd.tensor_scalar(out=am1_lo[:], in0=cols_lo[:, 4:8], scalar1=-1.0, scalar2=None, op0=ALU.add)
+        turned_factors = bank(BACK_BANKS)
+        nc.tensor.transpose(turned_factors[:, 0:P], factor_rows[:], ident[:])
+        factors_first = buf([P, 2 * PACK], F32, "factors_first")
+        nc.scalar.copy(out=factors_first[:], in_=turned_factors[:, 0:2 * PACK])
+        slope_first = buf([P, PACK], F32, "slope_first")
+        nc.gpsimd.tensor_scalar(out=slope_first[:], in0=factors_first[:, PACK:2 * PACK], scalar1=-1.0, scalar2=None,
+                                op0=ALU.add)
+        slope_second = buf([P, PACK - 1], F32, "slope_second")
+        nc.gpsimd.tensor_scalar(out=slope_second[:], in0=amp_second[:, 0:PACK - 1], scalar1=-1.0, scalar2=None,
+                                op0=ALU.add)
 
-        am1_hi = buf([P, 3], F32, "am1_hi")
-        nc.gpsimd.tensor_scalar(out=am1_hi[:], in0=amp_hi[:, 0:3], scalar1=-1.0, scalar2=None, op0=ALU.add)
         earlier = {}
-        after_page = {}
-        after_w1 = []
-        first_three = buf([P, 3 * BANK], F32, "first_three")
 
-        def fetch_earlier(s, h):
-            if 2 * s + h < 3:
-                e = first_three[:, half(2 * s + h)]
-            elif s == 1:
-                e = after_w1[0][:, half(1)]
-            elif s == 2 or h == 1:
-                e = after_page[s - 2][:, half(h)]
-            else:
-                e = buf([P, BANK], F32, "ring%d" % ((s - 3) % RING))[:]
+        def fetch_earlier(s, h, dst):
             looked_up = pages[s][:].indirect(half_list(idx4, h))
             if s == LAST:
-                nc.vector.tensor_copy(out=e, in_=looked_up)
+                nc.vector.tensor_copy(out=dst, in_=looked_up)
             else:
-                nc.vector.tensor_scalar(out=e, in0=looked_up, scalar1=-1.0, scalar2=0.0, op0=ALU.mult, op1=ALU.add)
-            earlier[s, h] = e
+                nc.vector.tensor_scalar(out=dst, in0=looked_up, scalar1=-1.0, scalar2=0.0, op0=ALU.mult, op1=ALU.add)
+            earlier[s, h] = dst
 
-        w1_codes = {}
+        w1_q = {}
 
-        def quantise_w1_slice(s):
-            raw = raw_lo[s]
-            grouped = buf([P, KP, P * 4], BF16, ["slot2", "slot1", "ring0", "ring1"][s])
-            for a in range(KP):
-                nc.scalar.copy(out=grouped[:, a, :].rearrange("p (c i j) -> p c j i", i=4, j=4),
-                               in_=raw[:, a, :, :].rearrange("p j (c i) -> p c j i", i=4))
-            codes = buf([P, KP * P], U32, "w1c%d" % s)
-            scales = buf([P, KP * P], U8, "w1s%d" % s)
+        def quantise_w1_slice(s, tag):
+            grouped = buf([P, K_PASSES, P * PACK], BF16, tag)
+            for a in range(K_PASSES):
+                nc.scalar.copy(out=grouped[:, a, :].rearrange("p (c i j) -> p c j i", i=4, j=PACK),
+                               in_=w1_slice_raw[s][:, a, :, :].rearrange("p j (c i) -> p c j i", i=4))
+            codes = buf([P, K_PASSES * P], U32, "w1_codes%d" % s)
+            scales = buf([P, K_PASSES * P], U8, "w1_scales%d" % s)
             nc.vector.quantize_mx(out=codes[:].bitcast(FP8X4), scales=scales[:],
                                   in_=grouped[:].rearrange("p a w -> p (a w)"))
-            w1_codes[s] = [(codes[:, blk(a)], scales[:, blk(a)]) for a in range(KP)]
+            w1_q[s] = [(codes[:, blk(a)], scales[:, blk(a)]) for a in range(K_PASSES)]
 
-        fetch_earlier(0, 0)
-        fetch_earlier(0, 1)
+        w1_second_q = []
+
+        def quantise_w1_second(a, tag):
+            grouped = buf([P, PASS * PACK], BF16, tag)
+            for g in range(4):
+                part = slice(32 * g, 32 * g + 32)
+                nc.scalar.copy(out=grouped[:].rearrange("p (t m j) -> p m j t", t=PACK, j=PACK)[:, part, :, :],
+                               in_=w1_second_raw[a][:].rearrange("p j (m t) -> p m j t", t=PACK)[:, part, :, :])
+            codes = buf([P, PASS], U32, "w1_second_codes%d" % a)
+            scales = buf([P, PASS], U8, "w1_second_scales%d" % a)
+            nc.vector.quantize_mx(out=codes[:].bitcast(FP8X4), scales=scales[:], in_=grouped[:])
+            w1_second_q.append((codes, scales))
+
+        w3_q = []
+
+        def quantise_w3(b, tag):
+            grouped = buf([P, N * PACK], BF16, tag)
+            for n in range(N // P):
+                part = slice(32 * n, 32 * n + 32)
+                nc.scalar.copy(out=grouped[:].rearrange("p (c i j) -> p c j i", i=4, j=PACK)[:, part, :, :],
+                               in_=w3_raw[b][:].rearrange("p j (c i) -> p c j i", i=4)[:, part, :, :])
+            codes = buf([P, N], U32, "w3_codes%d" % b)
+            scales = buf([P, N], U8, "w3_scales%d" % b)
+            nc.vector.quantize_mx(out=codes[:].bitcast(FP8X4), scales=scales[:], in_=grouped[:])
+            w3_q.append((codes, scales))
+
+        earlier_first = buf([P, 3 * BANK], F32, "earlier_first")
+        fetch_earlier(0, 0, earlier_first[:, half(0)])
+        fetch_earlier(0, 1, earlier_first[:, half(1)])
         v_sc = buf([P, S], U8, "v_sc")
         nc.vector.tensor_copy(out=v_sc[:], in_=tab_sc[:].indirect(idx[:]))
-        v = {}
-        for a in range(KP):
-            v[a] = buf([P, S], U32, "v%d" % a)
-            if a < KP - 1:
-                nc.vector.tensor_copy(out=v[a][:], in_=tab[a][:].indirect(idx[:]))
-            else:
-                for h in range(2):
-                    nc.vector.tensor_copy(out=v[a][:, half(h)], in_=tab[a][:].indirect(half_list(idx, h)))
-            if a == 0:
-                quantise_w1_slice(0)
+        v = [buf([P, S], U32, "v%d" % a) for a in range(K_PASSES)]
+        nc.vector.tensor_copy(out=v[0][:], in_=tab[0][:].indirect(idx[:]))
+        quantise_w1_slice(0, "slot2")
+        nc.vector.tensor_copy(out=v[1][:], in_=tab[1][:].indirect(idx[:]))
+        for h in range(2):
+            nc.vector.tensor_copy(out=v[2][:, half(h)], in_=tab[2][:].indirect(half_list(idx, h)))
 
-        habs = {}
-        wg = {}
-        dealt = {}
-
-        def load_dealt(t):
-            dealt[t] = buf([P, S], F32, ["ring4", "dealt0", "dealt1", "dealt0"][t])
-            rows = wgs.rearrange("(q t) j -> q t j", t=4)[:, t, :]
-            nc.sync.dma_start(out=dealt[t][:], in_=rows.partition_broadcast(4))
+        magnitude = {}
 
         def features(s):
-            hab = buf([P, S], F32, "habs%d" % (s % 3))
+            if s < PACK:
+                weights = w1_q[s]
+            else:
+                weights = [(codes[:, blk(s - PACK)], scales[:, blk(s - PACK)]) for codes, scales in w1_second_q]
+            magnitude[s] = buf([P, S], F32, "magnitude%d" % (s % FEATURE_BUFFERS))
             for h in range(2):
-                acc = bank(h if s in (0, 2) else 2 + h)
-                for n, a in enumerate(range(KP) if s == 0 else reversed(range(KP))):
-                    codes, scales = w1_codes[s][a]
+                acc = bank(FEATURE_BANKS[s] + h)
+                for step, a in enumerate(range(K_PASSES) if s == 0 else reversed(range(K_PASSES))):
+                    codes, scales = weights[a]
                     nc.tensor.matmul_mx(out=acc[:], lhsT=codes.bitcast(FP8X4), lhsT_scale=scales,
                                         rhs=v[a][:, half(h)].bitcast(FP8X4), rhs_scale=v_sc[4 * a:P, half(h)],
-                                        start=(n == 0), stop=(n == KP - 1))
-                nc.scalar.activation(out=hab[:, half(h)], in_=acc[:], func=ACT.Abs)
-            habs[s] = hab
+                                        start=(step == 0), stop=(step == K_PASSES - 1))
+                nc.scalar.activation(out=magnitude[s][:, half(h)], in_=acc[:], func=ACT.Abs)
 
-        def gained_weights(s):
-            w = after_page[s - 1][:, M:]
-            if s < 4:
-                nc.scalar.activation(out=w, in_=wgs_lo[:], func=ACT.Copy, scale=cols_lo[:, s:s + 1])
+        wgs_second = {}
+
+        def load_wgs_second(t, tag):
+            wgs_second[t] = buf([P, S], F32, tag)
+            rows = wgs.rearrange("(q t) j -> q t j", t=PACK)[:, t, :]
+            nc.sync.dma_start(out=wgs_second[t][:], in_=rows.partition_broadcast(QUADS))
+
+        def put_first(h, weight):
+            nc.scalar.activation(out=weight, in_=wgs_first[:, half(h)], func=ACT.Copy, scale=factors_first[:, 0:1])
+            nc.vector.tensor_tensor(pages[0][:].indirect(half_list(idx2, h)), magnitude[0][:, half(h)], weight, ALU.mult)
+
+        def gained_weights(s, dst):
+            if s < PACK:
+                nc.scalar.activation(out=dst, in_=wgs_first[:], func=ACT.Copy, scale=factors_first[:, s:s + 1])
             else:
-                nc.scalar.activation(out=w, in_=dealt[s - 4][:], func=ACT.Copy, scale=gain_hi[:, s - 4:s - 3])
-            wg[s] = w
+                nc.scalar.activation(out=dst, in_=wgs_second[s - PACK][:], func=ACT.Copy,
+                                     scale=gain_second[:, s - PACK:s - PACK + 1])
 
-        def put_first(h, w):
-            nc.scalar.activation(out=w, in_=wgs_lo[:, half(h)], func=ACT.Copy, scale=cols_lo[:, 0:1])
-            nc.vector.tensor_tensor(pages[0][:].indirect(half_list(idx2, h)), habs[0][:, half(h)], w, ALU.mult)
+        def put(s, weight):
+            nc.vector.tensor_tensor(pages[s][:].indirect(idx2[:]), magnitude[s][:], weight, ALU.mult)
 
-        def put(s):
-            nc.vector.tensor_tensor(pages[s][:].indirect(idx2[:]), habs[s][:], wg[s], ALU.mult)
-
-        xq = [(buf([P, M], U32, "xq%d" % b), buf([P, M], U8, "xs%d" % b)) for b in range(HP)]
-        planes = [buf([P, 4, BANK], BF16, "plane%d" % h) for h in range(2)]
-        turned_parts = {}
+        x_q = [(buf([P, M], U32, "x_codes%d" % b), buf([P, M], U8, "x_scales%d" % b)) for b in range(R_PASSES)]
+        planes = [buf([P, PACK, BANK], BF16, "plane%d" % h) for h in range(2)]
 
         def quantise_x(b, cols, grouped):
-            nc.vector.quantize_mx(out=xq[b][0][:, cols].bitcast(FP8X4), scales=xq[b][1][:, cols],
+            nc.vector.quantize_mx(out=x_q[b][0][:, cols].bitcast(FP8X4), scales=x_q[b][1][:, cols],
                                   in_=grouped[:].rearrange("p m t -> p (m t)"))
 
         def add_turned(dst, first, second):
             nc.tensor.matmul(dst, lhsT=first, rhs=ident[:], is_transpose=True, start=True, stop=False)
             nc.tensor.matmul(dst, lhsT=second, rhs=ident[:], is_transpose=True, start=False, stop=True)
 
-        changed = {}
-
-        def fetch_changed(s):
-            c = buf([P, M], F32, "ring%d" % (s % RING))
-            nc.vector.tensor_copy(out=c[:], in_=pages[s][:].indirect(idx3[:]))
-            changed[s] = c
-            if s < LAST:
-                after_page[s] = buf([P, T2], F32, "page%d" % PAGE_SLOT[s])
-
-        linear = {}
-
-        def scale_changed(s):
-            lin = buf([P, M], F32, "ring%d" % ((s + 1) % RING))
-            am1 = am1_lo[:, s:s + 1] if s < 4 else am1_hi[:, s - 4:s - 3]
+        def linear_part(s, changed):
+            linear = buf([P, M], F32, ring(s + 1))
+            slope = slope_first[:, s:s + 1] if s < PACK else slope_second[:, s - PACK:s - PACK + 1]
             for h in range(2):
-                nc.scalar.activation(out=lin[:, half(h)], in_=changed[s][:, half(h)], func=ACT.Copy, scale=am1)
-            linear[s] = lin
+                nc.scalar.activation(out=linear[:, half(h)], in_=changed[:, half(h)], func=ACT.Copy, scale=slope)
+            return linear
 
-        def compare(s):
-            c = changed[s]
-            lin = linear[s]
-            if s == 0:
-                turned_parts["over"] = buf([P, 8, 4, P], F32, "big0")
-                turned_parts["lin"] = buf([P, 8, 4, P], F32, "big1")
-            if s >= 4:
-                both = buf([P, 2, M], F32, "big2")
-                over_t, lin_t = both[:, 0, :], both[:, 1, :]
-            else:
-                over_t, lin_t = turned_parts["over"], turned_parts["lin"]
+        def turn(s, changed, linear):
+            banks = []
+            for h in range(2):
+                diff = bank(DIFF_BANKS + h)
+                for i in range(4):
+                    add_turned(diff[:, blk(i)], changed[:, blk(4 * h + i)], earlier[s, h][:, blk(i)])
+                turned_linear = bank(LINEAR_BANKS + h)
+                for i in range(4):
+                    nc.tensor.transpose(turned_linear[:, blk(i)], linear[:, blk(4 * h + i)], ident[:])
+                banks.append((diff, turned_linear))
+            return banks
 
-            def leave(dst, h, src, func):
-                if s < 4:
+        def leave_first(s, banks, parts):
+            for h in range(2):
+                for dst, src, func in zip(parts, banks[h], (ACT.Relu, ACT.Copy)):
                     nc.scalar.activation(out=dst[:, 4 * h:4 * h + 4, :, 32 * s:32 * s + 32],
-                                         in_=src[:].rearrange("p (b q t) -> p b t q", b=4, t=4), func=func)
-                else:
-                    nc.scalar.activation(out=dst[:, half(h)], in_=src[:], func=func)
+                                         in_=src[:].rearrange("p (b q t) -> p b t q", b=4, t=PACK), func=func)
 
+        def leave_second(banks):
+            both = buf([P, 2, M], F32, "big2")
+            parts = (both[:, 0, :], both[:, 1, :])
             for h in range(2):
-                diff = bank(2 + h)
-                for i in range(4):
-                    add_turned(diff[:, blk(i)], c[:, blk(4 * h + i)], earlier[s, h][:, blk(i)])
-                leave(over_t, h, diff, ACT.Relu)
-                lin_bank = bank(4 + h)
-                for i in range(4):
-                    nc.tensor.transpose(lin_bank[:, blk(i)], lin[:, blk(4 * h + i)], ident[:])
-                leave(lin_t, h, lin_bank, ACT.Copy)
-            if s == 3:
-                first_block_back([0, 1], [6, 7], "ring4")
-            if s == 4:
-                first_block_back([2, 3, 4], [0, 1, 6], "ring0")
-            if s == 5:
-                first_block_back([5, 6, 7], [6, 7, 1], "ring1")
-            if s >= 4:
-                for h in range(2):
-                    back = bank({4: [7, 0], 5: [0, 1], 6: [6, 7]}[s][h])
-                    for i in range(4):
-                        add_turned(back[:, blk(i)], over_t[:, blk(4 * h + i)], lin_t[:, blk(4 * h + i)])
-                    nc.scalar.copy(out=planes[h][:, s - 4, :], in_=back[:])
+                for dst, src, func in zip(parts, banks[h], (ACT.Relu, ACT.Copy)):
+                    nc.scalar.activation(out=dst[:, half(h)], in_=src[:], func=func)
+            return parts
 
-        def first_block_back(blocks, banks, tag):
-            over_t, lin_t = turned_parts["over"], turned_parts["lin"]
-            grouped = buf([P, len(blocks) * P, 4], BF16, tag)
-            for i, mb in enumerate(blocks):
-                back = bank(banks[i % len(banks)])
-                for t in range(4):
-                    add_turned(back[:, blk(t)], over_t[:, mb, t, :], lin_t[:, mb, t, :])
-                nc.scalar.copy(out=grouped[:, blk(i), :], in_=back[:].rearrange("p (t m) -> p m t", t=4))
-            quantise_x(0, slice(blocks[0] * P, (blocks[-1] + 1) * P), grouped)
+        def first_block_back(parts, pair, first_bank, tag):
+            grouped = buf([P, 2 * P, PACK], BF16, tag)
+            for i in range(2):
+                back = bank(first_bank + i)
+                for t in range(PACK):
+                    add_turned(back[:, blk(t)], parts[0][:, 2 * pair + i, t, :], parts[1][:, 2 * pair + i, t, :])
+                nc.scalar.copy(out=grouped[:, blk(i), :], in_=back[:].rearrange("p (t m) -> p m t", t=PACK))
+            quantise_x(0, slice(2 * pair * P, 2 * (pair + 1) * P), grouped)
 
-        def compare_last(h, last_changed):
-            s = LAST
-            c = last_changed[:, half(h)]
-            nc.vector.tensor_copy(out=c, in_=pages[s][:].indirect(half_list(idx3, h)))
+        def second_block_back(s, parts):
+            for h in range(2):
+                back = bank(BACK_BANKS + h)
+                for i in range(4):
+                    add_turned(back[:, blk(i)], parts[0][:, blk(4 * h + i)], parts[1][:, blk(4 * h + i)])
+                nc.scalar.copy(out=planes[h][:, s - PACK, :], in_=back[:])
+
+        def compare_last(h, changed):
+            nc.vector.tensor_copy(out=changed, in_=pages[LAST][:].indirect(half_list(idx3, h)))
             low = buf([P, BANK], F32, "raw%d" % h)
-            nc.vector.tensor_tensor(low[:], c, earlier[s, h], ALU.min)
-            nc.vector.scalar_tensor_tensor(out=planes[h][:, 3, :], in0=c, scalar=amp_hi[:, 3:4], in1=low[:],
-                                           op0=ALU.mult, op1=ALU.subtract)
-            grouped = buf([P, BANK, 4], BF16, ["slot1", "slot2"][h])
-            weave = nc.scalar.copy if h == 1 else nc.vector.tensor_copy
-            weave(out=grouped[:].rearrange("p (c i) t -> p c t i", i=4),
-                  in_=planes[h][:].rearrange("p t (c i) -> p c t i", i=4))
+            nc.vector.tensor_tensor(low[:], changed, earlier[LAST, h], ALU.min)
+            nc.vector.scalar_tensor_tensor(out=planes[h][:, PACK - 1, :], in0=changed, scalar=amp_second[:, PACK - 1:PACK],
+                                           in1=low[:], op0=ALU.mult, op1=ALU.subtract)
+            grouped = buf([P, BANK, PACK], BF16, "slot%d" % (1 + h))
+            interleave = nc.scalar.copy if h == 1 else nc.vector.tensor_copy
+            interleave(out=grouped[:].rearrange("p (c i) t -> p c t i", i=4),
+                       in_=planes[h][:].rearrange("p t (c i) -> p c t i", i=4))
             return grouped
 
-        hi_passes = []
-
-        def quantise_w1_hi(a):
-            grouped = buf([P, PASS * 4], BF16, ["slot2", "slot2", "ring2"][a])
-            for g in range(4):
-                nc.scalar.copy(out=grouped[:].rearrange("p (t m j) -> p m j t", t=4, j=4)[:, 32 * g:32 * g + 32, :, :],
-                               in_=raw_hi[a][:].rearrange("p j (m t) -> p m j t", t=4)[:, 32 * g:32 * g + 32, :, :])
-            codes = buf([P, PASS], U32, "w1hc%d" % a)
-            scales = buf([P, PASS], U8, "w1hs%d" % a)
-            nc.vector.quantize_mx(out=codes[:].bitcast(FP8X4), scales=scales[:], in_=grouped[:])
-            hi_passes.append((codes, scales))
-            if a == KP - 1:
-                for t in range(4):
-                    w1_codes[4 + t] = [(c[:, blk(t)], sc[:, blk(t)]) for c, sc in hi_passes]
-
-        w3_q = []
-        w4_w = []
-
-        def quantise_w3():
-            both = buf([P, HP, N * 4], BF16, "ring3")
-            all_codes = buf([P, HP * N], U32, "w3c")
-            for b in range(HP):
-                raw = buf([P, 4, N], F32, "raw%d" % b)
-                nc.sync.dma_start(out=raw[:], in_=w3[b * PASS:(b + 1) * PASS, :].rearrange("(p j) n -> p j n", j=4))
-                for g in range(3):
-                    nc.scalar.copy(out=both[:, b, :].rearrange("p (c i j) -> p c j i", i=4, j=4)[:, 32 * g:32 * g + 32, :, :],
-                                   in_=raw[:].rearrange("p j (c i) -> p c j i", i=4)[:, 32 * g:32 * g + 32, :, :])
-                codes = all_codes[:, b * N:(b + 1) * N]
-                scales = buf([P, N], U8, "w3s%d" % b)
-                nc.vector.quantize_mx(out=codes.bitcast(FP8X4), scales=scales[:], in_=both[:, b, :])
-                w3_q.append((codes, scales))
-
-        def load_w4_words():
-            words = buf([P, HP * 2 * N], U8, "page%d" % PAGE_SLOT[LAST])
-            for b in range(HP):
-                w4_w.append(words[:, b * 2 * N:(b + 1) * 2 * N])
-                nc.sync.dma_start(out=w4_w[b].bitcast(I32), in_=w4_words[b].bitcast(I32))
-
-        def load_w4_scales():
-            for q in range(4):
-                nc.sync.dma_start(out=w4_sc[32 * q:32 * q + 4, :].bitcast(I32).rearrange("r (b n) -> r b n", b=HP),
-                                  in_=w4_scales[:, 4 * q:4 * q + 4, :].bitcast(I32).rearrange("b r n -> r b n"))
-
         features(0)
-        put_first(0, buf([P, BANK], F32, "wg0")[:])
-        fetch_earlier(1, 0)
-        quantise_w1_slice(1)
-        after_w1.append(buf([P, M], F32, "slot1"))
-        fetch_earlier(1, 1)
-        put_first(1, after_w1[0][:, half(0)])
+        put_first(0, buf([P, BANK], F32, "weight_first")[:])
+        fetch_earlier(1, 0, earlier_first[:, half(2)])
+        quantise_w1_slice(1, "slot1")
+        after_w1 = buf([P, M], F32, "slot1")
+        fetch_earlier(1, 1, after_w1[:, half(1)])
+        put_first(1, after_w1[:, half(0)])
         features(1)
-        quantise_w1_slice(2)
+        quantise_w1_slice(2, ring(0))
         features(2)
-        load_dealt(0)
-        load_dealt(1)
-        for s in range(SLICES):
-            if s > 0:
-                put(s)
-            if s == LAST:
-                break
-            if 1 <= s < SLICES - 2:
-                fetch_earlier(s + 2, 0)
-            fetch_changed(s)
-            gained_weights(s + 1)
-            scale_changed(s)
-            if s == 0:
-                fetch_earlier(2, 0)
-            if s + 2 < SLICES:
-                fetch_earlier(s + 2, 1)
-            compare(s)
-            if s == 0:
-                quantise_w1_hi(0)
-                quantise_w1_slice(3)
-            if s == 1:
-                quantise_w1_hi(1)
-                quantise_w1_hi(2)
-            if s in (2, 3):
-                load_page(s + 4)
-            if s == 2:
-                quantise_w3()
-            if s in (3, 4):
-                load_dealt(s - 1)
-            for ahead in [[], [3], [4, 5], [6], [7], [], []][s]:
-                features(ahead)
-            if s == 5:
-                load_w4_scales()
 
-        all_bounded = buf([P, 6 * BANK], F32, "big0")
-        all_results = buf([P, 6 * BANK], F32, "big1")
-        order = [0, 1, 2, 3, 4, 5, 6, 7, 0, 1, 2, 3]
-        last_changed = buf([P, M], F32, "ring%d" % (LAST % RING))
-        last_x = {h: compare_last(h, last_changed) for h in (1, 0)}
-        load_w4_words()
+        first_parts = []
+        for s in range(LAST):
+            if 1 <= s < LAST - 2:
+                fetch_earlier(s + 2, 0, buf([P, BANK], F32, ring(s - 1))[:])
+            if s == LAST - 1:
+                fetch_earlier(LAST, 0, buf([P, BANK], F32, ring(s - 1))[:])
+            changed = buf([P, M], F32, ring(s))
+            nc.vector.tensor_copy(out=changed[:], in_=pages[s][:].indirect(idx3[:]))
+            after_page = buf([P, T2], F32, page_buffer(s))
+            weight = after_page[:, M:]
+            gained_weights(s + 1, weight)
+            linear = linear_part(s, changed)
+            if s == 0:
+                fetch_earlier(2, 0, after_page[:, half(0)])
+            if s + 2 < SLICES:
+                fetch_earlier(s + 2, 1, after_page[:, half(1)])
+            banks = turn(s, changed, linear)
+
+            if s == 0:
+                quantise_w1_slice(3, ring(s + 1))
+            if s == 1:
+                quantise_w1_second(1, ring(s + 1))
+            if s + PACK >= PAGE_BUFFERS and s + PACK < SLICES:
+                load_page(s + PACK)
+            if s == 2:
+                quantise_w3(0, ring(s + 1))
+            if s >= PACK:
+                first_block_back(first_parts, s - PACK + 1, SPARE_BANKS, ring(s + 1))
+            if s == 0:
+                first_parts = [buf([P, M // P, PACK, P], F32, "big0"), buf([P, M // P, PACK, P], F32, "big1")]
+            if s < PACK:
+                leave_first(s, banks, first_parts)
+            else:
+                second_block_back(s, leave_second(banks))
+            if s == PACK - 1:
+                first_block_back(first_parts, 0, BACK_BANKS, ring(s + 1))
+
+            if s == 0:
+                quantise_w1_second(0, ring(PACK))
+                load_wgs_second(0, ring(PACK))
+            if s == 1:
+                quantise_w1_second(2, "slot2")
+                load_wgs_second(1, "slot2")
+                load_wgs_second(2, "raw1")
+                features(3)
+            if s == 2:
+                features(4)
+            if s == 3:
+                quantise_w3(1, "w3_grouped")
+            if s == 4:
+                load_wgs_second(3, "slot2")
+            if 2 <= s <= 4:
+                features(s + 3)
+            if s == 5:
+                for q in range(QUADS):
+                    nc.sync.dma_start(
+                        out=w4_sc[32 * q:32 * q + 4, :].bitcast(I32).rearrange("r (b n) -> r b n", b=R_PASSES),
+                        in_=w4_scales[:, 4 * q:4 * q + 4, :].bitcast(I32).rearrange("b r n -> r b n"))
+            put(s + 1, weight)
+
+        groups = 2 * (N // P)
+        all_bounded = buf([P, groups * BANK], F32, "big0")
+        all_results = buf([P, groups * BANK], F32, "big1")
+        last_changed = buf([P, M], F32, ring(LAST))
+        last_x = {h: compare_last(h, last_changed[:, half(h)]) for h in (1, 0)}
+        w4_all = buf([P, R_PASSES * 2 * N], U8, page_buffer(LAST))
+        w4_w = [w4_all[:, b * 2 * N:(b + 1) * 2 * N] for b in range(R_PASSES)]
+        for b in range(R_PASSES):
+            nc.sync.dma_start(out=w4_w[b].bitcast(I32), in_=w4_words[b].bitcast(I32))
         for h in range(2):
             quantise_x(1, half(h), last_x[h])
         for h in range(2):
             for n in range(N // P):
-                g = 2 * (h * (N // P) + n)
-                y4 = bank(order[g])
-                for b in range(HP):
+                g = h * (N // P) + n
+                y4 = bank(2 * g % 8)
+                for b in range(R_PASSES):
                     nc.tensor.matmul_mx(out=y4[:], lhsT=w4_w[b][:, 2 * n * P:2 * (n + 1) * P].bitcast(FP4X4),
                                         lhsT_scale=w4_sc[:, b * N + n * P:b * N + (n + 1) * P],
-                                        rhs=xq[b][0][:, half(h)].bitcast(FP8X4), rhs_scale=xq[b][1][:, half(h)],
-                                        start=(b == 0), stop=(b == HP - 1))
-                y3 = bank(order[g + 1])
-                for b in range(HP):
+                                        rhs=x_q[b][0][:, half(h)].bitcast(FP8X4), rhs_scale=x_q[b][1][:, half(h)],
+                                        start=(b == 0), stop=(b == R_PASSES - 1))
+                y3 = bank((2 * g + 1) % 8)
+                for b in range(R_PASSES):
                     nc.tensor.matmul_mx(out=y3[:], lhsT=w3_q[b][0][:, blk(n)].bitcast(FP8X4),
                                         lhsT_scale=w3_q[b][1][:, blk(n)],
-                                        rhs=xq[b][0][:, half(h)].bitcast(FP8X4), rhs_scale=xq[b][1][:, half(h)],
-                                        start=(b == 0), stop=(b == HP - 1))
-                bounded = all_bounded[:, half(g // 2)]
+                                        rhs=x_q[b][0][:, half(h)].bitcast(FP8X4), rhs_scale=x_q[b][1][:, half(h)],
+                                        start=(b == 0), stop=(b == R_PASSES - 1))
+                bounded = all_bounded[:, g * BANK:(g + 1) * BANK]
                 nc.scalar.activation(out=bounded, in_=y4[:], func=ACT.Tanh)
-                result = all_results[:, half(g // 2)]
+                result = all_results[:, g * BANK:(g + 1) * BANK]
                 nc.vector.tensor_tensor(result, y3[:], bounded, ALU.add)
                 nc.sync.dma_start(out=out[blk(n), half(h)], in_=result)

from contextlib import ExitStack

import concourse.mybir as mybir
from concourse.masks import make_identity

K, H, N, T, S, T2, M = 1536, 1024, 384, 4096, 1024, 2048, 1024
FLOPS = 2 * K * H * S + 2 * 2 * H * N * M

F32 = mybir.dt.float32
BF16 = mybir.dt.bfloat16
I32 = mybir.dt.int32
U32 = mybir.dt.uint32
U16 = mybir.dt.uint16
U8 = mybir.dt.uint8
FP8X4 = mybir.dt.float8_e4m3fn_x4
FP4X4 = mybir.dt.float4_e2m1fn_x4
ALU = mybir.AluOpType
ACT = mybir.ActivationFunctionType

P = 128
PACK = 4
PASS = P * PACK
K_PASSES = K // PASS
R_PASSES = H // PASS
BANK = 512
QUADS = 4
SLICES = H // P
LAST = SLICES - 1
PAGE_BUFFERS = 6
FEATURE_BUFFERS = 3
RING = 5
SPARE_BANKS = 0
DIFF_BANKS = 2
LINEAR_BANKS = 4
BACK_BANKS = 6
FEATURE_BANKS = [SPARE_BANKS, DIFF_BANKS, SPARE_BANKS, SPARE_BANKS, SPARE_BANKS, DIFF_BANKS, BACK_BANKS, DIFF_BANKS]


def tile_list_bridge_wear_scores_kernel(tc, tab_words, tab_scales, offs, w1, gain, page0, wgs,
                                                  offs2, offs3, offs4, amp, w4_words, w4_scales, w3, out):
    nc = tc.nc
    with ExitStack() as ctx:
        lists = ctx.enter_context(tc.tile_pool(name="lists", bufs=1))
        sb = ctx.enter_context(tc.tile_pool(name="sb", bufs=1))
        ps = ctx.enter_context(tc.psum_pool(name="ps", bufs=1))

        def buf(shape, dtype, tag):
            return sb.tile(shape, dtype, tag=tag, name=tag, align_bytes=64)

        def ring(i):
            return "ring%d" % (i % RING)

        def page_buffer(s):
            return "page%d" % (s % PAGE_BUFFERS)

        def bank(b):
            return ps.tile([P, BANK], F32, tag="bank%d" % b, name="bank%d" % b)

        def load_list(src, name):
            entries = lists.tile([P, S // 16], U16, name=name)
            nc.sync.dma_start(entries[:], src)
            return entries

        def half(h):
            return slice(h * BANK, (h + 1) * BANK)

        def half_list(entries, h):
            return entries[:, h * (BANK // 16):(h + 1) * (BANK // 16)]

        def blk(i):
            return slice(i * P, (i + 1) * P)

        ident = buf([P, P], F32, "ident")
        make_identity(nc, ident[:])
        tab_sc = buf([P, T], U8, "tab_sc")
        nc.vector.memset(tab_sc[:].bitcast(I32), 0)
        factor_rows = buf([P, P], F32, "factor_rows")
        nc.vector.memset(factor_rows[:], 0.0)
        w4_sc = buf([P, R_PASSES * N], U8, "w4_sc")
        nc.vector.memset(w4_sc[:].bitcast(I32), 0)

        pages = {}

        def load_page(s):
            page = buf([P, T2], F32, page_buffer(s))
            if s < PACK:
                rows = page0[blk(s), :]
            else:
                rows = page0[PASS:, :].rearrange("(p t) c -> p t c", t=PACK)[:, s - PACK, :]
            nc.sync.dma_start(out=page[:], in_=rows)
            pages[s] = page

        tab = {}

        def load_table(a):
            words = buf([P, T], U32, "big%d" % a)
            nc.sync.dma_start(out=words[:].bitcast(I32),
                              in_=tab_words[a].rearrange("p t i -> p (t i)").bitcast(I32))
            tab[a] = words

        w1_slice_raw = {}

        def load_w1_slice(s, tag):
            raw = buf([P, K_PASSES, PACK, P], F32, tag)
            for a in range(K_PASSES):
                rows = w1[a * PASS:(a + 1) * PASS, blk(s)]
                nc.sync.dma_start(out=raw[:, a, :, :], in_=rows.rearrange("(p j) c -> p j c", j=PACK))
            w1_slice_raw[s] = raw

        def load_pass(weight, a, cols, tag):
            raw = buf([P, PACK, cols.stop - cols.start], F32, tag)
            nc.sync.dma_start(out=raw[:], in_=weight[a * PASS:(a + 1) * PASS, cols].rearrange("(p j) c -> p j c", j=PACK))
            return raw

        load_page(0)
        idx4 = load_list(offs4, "idx4")
        for q in range(QUADS):
            nc.sync.dma_start(out=tab_sc[32 * q:32 * q + 4 * K_PASSES, :].bitcast(I32),
                              in_=tab_scales[:, 4 * q:4 * q + 4, :].bitcast(I32))
        load_table(0)
        idx = load_list(offs, "idx")
        load_w1_slice(0, "raw0")
        load_table(1)
        nc.sync.dma_start(out=factor_rows[0:PACK, :], in_=gain[0:PASS].rearrange("(s p) -> s p", p=P))
        nc.sync.dma_start(out=factor_rows[PACK:2 * PACK, :], in_=amp[0:PASS].rearrange("(s p) -> s p", p=P))
        wgs_first = buf([P, S], F32, "wgs_first")
        nc.sync.dma_start(out=wgs_first[:, half(0)], in_=wgs[:, half(0)])
        load_table(2)
        nc.sync.dma_start(out=wgs_first[:, half(1)], in_=wgs[:, half(1)])
        idx2 = load_list(offs2, "idx2")
        load_page(1)
        load_w1_slice(1, "raw1")
        idx3 = load_list(offs3, "idx3")
        load_page(2)
        load_w1_slice(2, page_buffer(5))
        gain_second = buf([P, PACK], F32, "gain_second")
        nc.sync.dma_start(out=gain_second[:], in_=gain[PASS:].rearrange("(p t) -> p t", t=PACK))
        amp_second = buf([P, PACK], F32, "amp_second")
        nc.sync.dma_start(out=amp_second[:], in_=amp[PASS:].rearrange("(p t) -> p t", t=PACK))
        second_columns = slice(PASS, H)
        w1_second_raw = [load_pass(w1, 0, second_columns, "raw0")]
        load_page(3)
        load_w1_slice(3, "raw2")
        load_page(4)
        w1_second_raw.append(load_pass(w1, 1, second_columns, "raw1"))
        w1_second_raw.append(load_pass(w1, 2, second_columns, "big2"))
        load_page(5)
        w3_raw = [load_pass(w3, 0, slice(0, N), "raw2"), load_pass(w3, 1, slice(0, N), "raw0")]

        turned_factors = bank(BACK_BANKS)
        nc.tensor.transpose(turned_factors[:, 0:P], factor_rows[:], ident[:])
        factors_first = buf([P, 2 * PACK], F32, "factors_first")
        nc.scalar.copy(out=factors_first[:], in_=turned_factors[:, 0:2 * PACK])
        slope_first = buf([P, PACK], F32, "slope_first")
        nc.gpsimd.tensor_scalar(out=slope_first[:], in0=factors_first[:, PACK:2 * PACK], scalar1=-1.0, scalar2=None,
                                op0=ALU.add)
        slope_second = buf([P, PACK - 1], F32, "slope_second")
        nc.gpsimd.tensor_scalar(out=slope_second[:], in0=amp_second[:, 0:PACK - 1], scalar1=-1.0, scalar2=None,
                                op0=ALU.add)

        earlier = {}

        def fetch_earlier(s, h, dst):
            looked_up = pages[s][:].indirect(half_list(idx4, h))
            if s == LAST:
                nc.vector.tensor_copy(out=dst, in_=looked_up)
            else:
                nc.vector.tensor_scalar(out=dst, in0=looked_up, scalar1=-1.0, scalar2=0.0, op0=ALU.mult, op1=ALU.add)
            earlier[s, h] = dst

        w1_q = {}

        def quantise_w1_slice(s, tag):
            grouped = buf([P, K_PASSES, P * PACK], BF16, tag)
            for a in range(K_PASSES):
                nc.scalar.copy(out=grouped[:, a, :].rearrange("p (c i j) -> p c j i", i=4, j=PACK),
                               in_=w1_slice_raw[s][:, a, :, :].rearrange("p j (c i) -> p c j i", i=4))
            codes = buf([P, K_PASSES * P], U32, "w1_codes%d" % s)
            scales = buf([P, K_PASSES * P], U8, "w1_scales%d" % s)
            nc.vector.quantize_mx(out=codes[:].bitcast(FP8X4), scales=scales[:],
                                  in_=grouped[:].rearrange("p a w -> p (a w)"))
            w1_q[s] = [(codes[:, blk(a)], scales[:, blk(a)]) for a in range(K_PASSES)]

        w1_second_q = []

        def quantise_w1_second(a, tag):
            grouped = buf([P, PASS * PACK], BF16, tag)
            for g in range(4):
                part = slice(32 * g, 32 * g + 32)
                nc.scalar.copy(out=grouped[:].rearrange("p (t m j) -> p m j t", t=PACK, j=PACK)[:, part, :, :],
                               in_=w1_second_raw[a][:].rearrange("p j (m t) -> p m j t", t=PACK)[:, part, :, :])
            codes = buf([P, PASS], U32, "w1_second_codes%d" % a)
            scales = buf([P, PASS], U8, "w1_second_scales%d" % a)
            nc.vector.quantize_mx(out=codes[:].bitcast(FP8X4), scales=scales[:], in_=grouped[:])
            w1_second_q.append((codes, scales))

        w3_q = []

        def quantise_w3(b, tag):
            grouped = buf([P, N * PACK], BF16, tag)
            for n in range(N // P):
                part = slice(32 * n, 32 * n + 32)
                nc.scalar.copy(out=grouped[:].rearrange("p (c i j) -> p c j i", i=4, j=PACK)[:, part, :, :],
                               in_=w3_raw[b][:].rearrange("p j (c i) -> p c j i", i=4)[:, part, :, :])
            codes = buf([P, N], U32, "w3_codes%d" % b)
            scales = buf([P, N], U8, "w3_scales%d" % b)
            nc.vector.quantize_mx(out=codes[:].bitcast(FP8X4), scales=scales[:], in_=grouped[:])
            w3_q.append((codes, scales))

        earlier_first = buf([P, 3 * BANK], F32, "earlier_first")
        fetch_earlier(0, 0, earlier_first[:, half(0)])
        fetch_earlier(0, 1, earlier_first[:, half(1)])
        v_sc = buf([P, S], U8, "v_sc")
        nc.vector.tensor_copy(out=v_sc[:], in_=tab_sc[:].indirect(idx[:]))
        v = [buf([P, S], U32, "v%d" % a) for a in range(K_PASSES)]
        nc.vector.tensor_copy(out=v[0][:], in_=tab[0][:].indirect(idx[:]))
        quantise_w1_slice(0, "slot2")
        nc.vector.tensor_copy(out=v[1][:], in_=tab[1][:].indirect(idx[:]))
        for h in range(2):
            nc.vector.tensor_copy(out=v[2][:, half(h)], in_=tab[2][:].indirect(half_list(idx, h)))

        magnitude = {}

        def features(s):
            if s < PACK:
                weights = w1_q[s]
            else:
                weights = [(codes[:, blk(s - PACK)], scales[:, blk(s - PACK)]) for codes, scales in w1_second_q]
            magnitude[s] = buf([P, S], F32, "magnitude%d" % (s % FEATURE_BUFFERS))
            for h in range(2):
                acc = bank(FEATURE_BANKS[s] + h)
                for step, a in enumerate(range(K_PASSES) if s == 0 else reversed(range(K_PASSES))):
                    codes, scales = weights[a]
                    nc.tensor.matmul_mx(out=acc[:], lhsT=codes.bitcast(FP8X4), lhsT_scale=scales,
                                        rhs=v[a][:, half(h)].bitcast(FP8X4), rhs_scale=v_sc[4 * a:P, half(h)],
                                        start=(step == 0), stop=(step == K_PASSES - 1))
                nc.scalar.activation(out=magnitude[s][:, half(h)], in_=acc[:], func=ACT.Abs)

        wgs_second = {}

        def load_wgs_second(t, tag):
            wgs_second[t] = buf([P, S], F32, tag)
            rows = wgs.rearrange("(q t) j -> q t j", t=PACK)[:, t, :]
            nc.sync.dma_start(out=wgs_second[t][:], in_=rows.partition_broadcast(QUADS))

        def put_first(h, weight):
            nc.scalar.activation(out=weight, in_=wgs_first[:, half(h)], func=ACT.Copy, scale=factors_first[:, 0:1])
            nc.vector.tensor_tensor(pages[0][:].indirect(half_list(idx2, h)), magnitude[0][:, half(h)], weight, ALU.mult)

        def gained_weights(s, dst):
            if s < PACK:
                nc.scalar.activation(out=dst, in_=wgs_first[:], func=ACT.Copy, scale=factors_first[:, s:s + 1])
            else:
                nc.scalar.activation(out=dst, in_=wgs_second[s - PACK][:], func=ACT.Copy,
                                     scale=gain_second[:, s - PACK:s - PACK + 1])

        def put(s, weight):
            nc.vector.tensor_tensor(pages[s][:].indirect(idx2[:]), magnitude[s][:], weight, ALU.mult)

        x_q = [(buf([P, M], U32, "x_codes%d" % b), buf([P, M], U8, "x_scales%d" % b)) for b in range(R_PASSES)]
        planes = [buf([P, PACK, BANK], BF16, "plane%d" % h) for h in range(2)]

        def quantise_x(b, cols, grouped):
            nc.vector.quantize_mx(out=x_q[b][0][:, cols].bitcast(FP8X4), scales=x_q[b][1][:, cols],
                                  in_=grouped[:].rearrange("p m t -> p (m t)"))

        def add_turned(dst, first, second):
            nc.tensor.matmul(dst, lhsT=first, rhs=ident[:], is_transpose=True, start=True, stop=False)
            nc.tensor.matmul(dst, lhsT=second, rhs=ident[:], is_transpose=True, start=False, stop=True)

        def linear_part(s, changed):
            linear = buf([P, M], F32, ring(s + 1))
            slope = slope_first[:, s:s + 1] if s < PACK else slope_second[:, s - PACK:s - PACK + 1]
            for h in range(2):
                nc.scalar.activation(out=linear[:, half(h)], in_=changed[:, half(h)], func=ACT.Copy, scale=slope)
            return linear

        def turn(s, changed, linear):
            banks = []
            for h in range(2):
                diff = bank(DIFF_BANKS + h)
                for i in range(4):
                    add_turned(diff[:, blk(i)], changed[:, blk(4 * h + i)], earlier[s, h][:, blk(i)])
                turned_linear = bank(LINEAR_BANKS + h)
                for i in range(4):
                    nc.tensor.transpose(turned_linear[:, blk(i)], linear[:, blk(4 * h + i)], ident[:])
                banks.append((diff, turned_linear))
            return banks

        def leave_first(s, banks, parts):
            for h in range(2):
                for dst, src, func in zip(parts, banks[h], (ACT.Relu, ACT.Copy)):
                    nc.scalar.activation(out=dst[:, 4 * h:4 * h + 4, :, 32 * s:32 * s + 32],
                                         in_=src[:].rearrange("p (b q t) -> p b t q", b=4, t=PACK), func=func)

        def leave_second(banks):
            both = buf([P, 2, M], F32, "big2")
            parts = (both[:, 0, :], both[:, 1, :])
            for h in range(2):
                for dst, src, func in zip(parts, banks[h], (ACT.Relu, ACT.Copy)):
                    nc.scalar.activation(out=dst[:, half(h)], in_=src[:], func=func)
            return parts

        def first_block_back(parts, pair, first_bank, tag):
            grouped = buf([P, 2 * P, PACK], BF16, tag)
            for i in range(2):
                back = bank(first_bank + i)
                for t in range(PACK):
                    add_turned(back[:, blk(t)], parts[0][:, 2 * pair + i, t, :], parts[1][:, 2 * pair + i, t, :])
                nc.scalar.copy(out=grouped[:, blk(i), :], in_=back[:].rearrange("p (t m) -> p m t", t=PACK))
            quantise_x(0, slice(2 * pair * P, 2 * (pair + 1) * P), grouped)

        def second_block_back(s, parts):
            for h in range(2):
                back = bank(BACK_BANKS + h)
                for i in range(4):
                    add_turned(back[:, blk(i)], parts[0][:, blk(4 * h + i)], parts[1][:, blk(4 * h + i)])
                nc.scalar.copy(out=planes[h][:, s - PACK, :], in_=back[:])

        def compare_last(h, changed):
            nc.vector.tensor_copy(out=changed, in_=pages[LAST][:].indirect(half_list(idx3, h)))
            low = buf([P, BANK], F32, "raw%d" % h)
            nc.vector.tensor_tensor(low[:], changed, earlier[LAST, h], ALU.min)
            nc.vector.scalar_tensor_tensor(out=planes[h][:, PACK - 1, :], in0=changed, scalar=amp_second[:, PACK - 1:PACK],
                                           in1=low[:], op0=ALU.mult, op1=ALU.subtract)
            grouped = buf([P, BANK, PACK], BF16, "slot%d" % (1 + h))
            interleave = nc.scalar.copy if h == 1 else nc.vector.tensor_copy
            interleave(out=grouped[:].rearrange("p (c i) t -> p c t i", i=4),
                       in_=planes[h][:].rearrange("p t (c i) -> p c t i", i=4))
            return grouped

        features(0)
        put_first(0, buf([P, BANK], F32, "weight_first")[:])
        fetch_earlier(1, 0, earlier_first[:, half(2)])
        quantise_w1_slice(1, "slot1")
        after_w1 = buf([P, M], F32, "slot1")
        fetch_earlier(1, 1, after_w1[:, half(1)])
        put_first(1, after_w1[:, half(0)])
        features(1)
        quantise_w1_slice(2, ring(0))
        features(2)

        first_parts = []
        for s in range(LAST):
            if 1 <= s < LAST - 2:
                fetch_earlier(s + 2, 0, buf([P, BANK], F32, ring(s - 1))[:])
            if s == LAST - 1:
                fetch_earlier(LAST, 0, buf([P, BANK], F32, ring(s - 1))[:])
            changed = buf([P, M], F32, ring(s))
            nc.vector.tensor_copy(out=changed[:], in_=pages[s][:].indirect(idx3[:]))
            after_page = buf([P, T2], F32, page_buffer(s))
            weight = after_page[:, M:]
            gained_weights(s + 1, weight)
            linear = linear_part(s, changed)
            if s == 0:
                fetch_earlier(2, 0, after_page[:, half(0)])
            if s + 2 < SLICES:
                fetch_earlier(s + 2, 1, after_page[:, half(1)])
            banks = turn(s, changed, linear)

            if s == 0:
                quantise_w1_slice(3, ring(s + 1))
            if s == 1:
                quantise_w1_second(1, ring(s + 1))
            if s + PACK >= PAGE_BUFFERS and s + PACK < SLICES:
                load_page(s + PACK)
            if s == 2:
                quantise_w3(0, ring(s + 1))
            if s >= PACK:
                first_block_back(first_parts, s - PACK + 1, SPARE_BANKS, ring(s + 1))
            if s == 0:
                first_parts = [buf([P, M // P, PACK, P], F32, "big0"), buf([P, M // P, PACK, P], F32, "big1")]
            if s < PACK:
                leave_first(s, banks, first_parts)
            else:
                second_block_back(s, leave_second(banks))
            if s == PACK - 1:
                first_block_back(first_parts, 0, BACK_BANKS, ring(s + 1))

            if s == 0:
                quantise_w1_second(0, ring(PACK))
                load_wgs_second(0, ring(PACK))
            if s == 1:
                quantise_w1_second(2, "slot2")
                load_wgs_second(1, "slot2")
                load_wgs_second(2, "raw1")
                features(3)
            if s == 2:
                features(4)
            if s == 3:
                quantise_w3(1, "w3_grouped")
            if s == 4:
                load_wgs_second(3, "slot2")
            if 2 <= s <= 4:
                features(s + 3)
            if s == 5:
                for q in range(QUADS):
                    nc.sync.dma_start(
                        out=w4_sc[32 * q:32 * q + 4, :].bitcast(I32).rearrange("r (b n) -> r b n", b=R_PASSES),
                        in_=w4_scales[:, 4 * q:4 * q + 4, :].bitcast(I32).rearrange("b r n -> r b n"))
            put(s + 1, weight)

        groups = 2 * (N // P)
        all_bounded = buf([P, groups * BANK], F32, "big0")
        all_results = buf([P, groups * BANK], F32, "big1")
        last_changed = buf([P, M], F32, ring(LAST))
        last_x = {h: compare_last(h, last_changed[:, half(h)]) for h in (1, 0)}
        w4_all = buf([P, R_PASSES * 2 * N], U8, page_buffer(LAST))
        w4_w = [w4_all[:, b * 2 * N:(b + 1) * 2 * N] for b in range(R_PASSES)]
        for b in range(R_PASSES):
            nc.sync.dma_start(out=w4_w[b].bitcast(I32), in_=w4_words[b].bitcast(I32))
        for h in range(2):
            quantise_x(1, half(h), last_x[h])
        for h in range(2):
            for n in range(N // P):
                g = h * (N // P) + n
                y4 = bank(2 * g % 8)
                for b in range(R_PASSES):
                    nc.tensor.matmul_mx(out=y4[:], lhsT=w4_w[b][:, 2 * n * P:2 * (n + 1) * P].bitcast(FP4X4),
                                        lhsT_scale=w4_sc[:, b * N + n * P:b * N + (n + 1) * P],
                                        rhs=x_q[b][0][:, half(h)].bitcast(FP8X4), rhs_scale=x_q[b][1][:, half(h)],
                                        start=(b == 0), stop=(b == R_PASSES - 1))
                y3 = bank((2 * g + 1) % 8)
                for b in range(R_PASSES):
                    nc.tensor.matmul_mx(out=y3[:], lhsT=w3_q[b][0][:, blk(n)].bitcast(FP8X4),
                                        lhsT_scale=w3_q[b][1][:, blk(n)],
                                        rhs=x_q[b][0][:, half(h)].bitcast(FP8X4), rhs_scale=x_q[b][1][:, half(h)],
                                        start=(b == 0), stop=(b == R_PASSES - 1))
                bounded = all_bounded[:, g * BANK:(g + 1) * BANK]
                nc.scalar.activation(out=bounded, in_=y4[:], func=ACT.Tanh)
                result = all_results[:, g * BANK:(g + 1) * BANK]
                nc.vector.tensor_tensor(result, y3[:], bounded, ALU.add)
                nc.sync.dma_start(out=out[blk(n), half(h)], in_=result)
